import numpy as np, ml_dtypes
CORES = [6,15,38,47]
N = 4
BF = ml_dtypes.bfloat16
S, D, H, CAP = 4096, 3, 64, 2048
def heads(x):
    return x.astype(np.float32).reshape(N, 8, 16, S)
def scores(z, v, t):
    return np.einsum("rgcs,rgc->rgs", z, v[:, :, t].astype(np.float32).reshape(N, 8, 16))
def layer(z, kept, w, gap, t):
    out = z.copy()
    for g in range(8):
        q = np.concatenate([z[r, g][:, kept[r][g]] for r in range(N)], axis=1)
        q = np.pad(q, ((0, 0), (H, H))); a = H
        for r in range(N):
            k = kept[r][g].size; d = int(gap[r, 16 * g, t])
            m = w[r, 16 * g:16 * g + 16, 48 * t:48 * t + 48].astype(np.float32)
            s = m[:, :16].T @ q[:, a:a + k] + m[:, 16:32].T @ q[:, a - d:a - d + k] + m[:, 32:].T @ q[:, a + d:a + d + k]
            out[r, g][:, kept[r][g]] = np.clip(np.rint(s * np.float32(0.125)), -15, 15)
            a += k
    return out
def run(x, v, w, th, gap):
    z = heads(x); kept = [[np.arange(S)] * 8 for r in range(N)]; cnt = np.zeros((D, N, 8), np.int64)
    for t in range(D):
        s = scores(z, v, t)
        kept = [[kept[r][g][s[r, g, kept[r][g]] >= th[r, 16 * g, t]] for g in range(8)] for r in range(N)]
        for r in range(N):
            for g in range(8): cnt[t, r, g] = kept[r][g].size
        z = layer(z, kept, w, gap, t)
    return z, cnt
def rows16(a):
    return np.repeat(a, 16, axis=1).astype(np.int32)
def shares(rng):
    k = [rng.integers(CAP // 2, CAP * 7 // 8 + 1, (N, 8))]
    for t in range(1, D): k.append(np.maximum(k[-1] * rng.integers(60, 91, (N, 8)) // 100, H))
    return np.stack(k)
def settle(d, want):
    x, v, w, gap = d["x"], d["v"], d["w"], d["gap"]
    z = heads(x); kept = [[np.arange(S)] * 8 for r in range(N)]; th = np.zeros((N, 8, D), np.int32)
    for t in range(D):
        s = scores(z, v, t)
        for r in range(N):
            for g in range(8):
                a = s[r, g, kept[r][g]]; e = np.sort(a)[::-1]; lim = int(e[min(int(want[t, r, g]), e.size) - 1])
                if np.count_nonzero(a >= lim) > CAP: lim += 1
                th[r, g, t] = lim; kept[r][g] = kept[r][g][a >= lim]
        z = layer(z, kept, w, gap, t)
    d["th"] = rows16(th); return d
def setup_inputs(rng):
    d = {"x": rng.integers(-15, 16, (N, 128, S)).astype(np.float32).astype(BF), "v": rng.integers(-7, 8, (N, 128, D)).astype(np.float32).astype(BF),
         "w": (2 * rng.integers(0, 2, (N, 128, 48 * D)) - 1).astype(np.float32).astype(BF), "th": None, "gap": rows16(rng.integers(1, H + 1, (N, 8, D)))}
    return settle(d, shares(rng))
def setup_inputs_caps(rng):
    d = setup_inputs(rng); x = d["x"]; s = scores(heads(x), d["v"], 0); g8 = np.arange(8)
    big = (np.arange(N)[:, None] + g8 + rng.integers(0, 2)) % 2 == 0
    for r in range(N):
        for g in range(8):
            k = CAP if big[r, g] else H; u = s[r, g]; o = np.argsort(-u, kind="stable"); late = o[k:]; late = late[u[late] == u[o[k - 1]]]
            b = x[r, 16 * g:16 * g + 16]; b[:, late] = b[:, o[-1:]]
    want = np.stack([np.where(big, CAP, H)] + [np.where(big & (g8 % 4 < 2), CAP, H)] * (D - 1))
    d["gap"] = rows16(rng.choice(np.array([1, H]), (N, 8, D))); return settle(d, want)
def setup_inputs_ends(rng):
    d = setup_inputs(rng); x = d["x"]; s = scores(heads(x), d["v"], 0); k = int(rng.integers(0, 3))
    for r in range(N):
        for g in range(8):
            o = np.argsort(-s[r, g], kind="stable"); m = (r + g + k) % 3
            if m == 1: o = o[::-1]
            if m == 2: o = np.concatenate([o[0::2], o[1::2][::-1]])
            x[r, 16 * g:16 * g + 16] = x[r, 16 * g:16 * g + 16][:, o]
    d["gap"] = rows16(rng.choice(np.array([1, H]), (N, 8, D))); return settle(d, shares(rng))
def setup_inputs_ties(rng):
    d = setup_inputs(rng); c = rng.integers(0, 16, (N, 8, 1, D)); sg = 2 * rng.integers(0, 2, (N, 8, 1, D)) - 1
    d["v"] = ((np.arange(16)[:, None] == c) * sg).reshape(N, 128, D).astype(np.float32).astype(BF)
    return settle(d, shares(rng))
def setup_inputs_spread(rng):
    d = setup_inputs(rng); m = rng.integers(0, 16, (N, 8, 1, S))
    d["x"] = np.rint((2 * rng.random((N, 8, 16, S)) - 1) * m).reshape(N, 128, S).astype(np.float32).astype(BF)
    return settle(d, shares(rng))
def check_inputs(d):
    bad = []; x, v, w = [np.asarray(d[k]).astype(np.float32) for k in ("x", "v", "w")]; th, gap = d["th"], d["gap"]
    if not ((np.rint(x) == x) & (np.abs(x) <= 15)).all(): bad.append("x_whole_within_15")
    if not ((np.rint(v) == v) & (np.abs(v) <= 7)).all(): bad.append("v_whole_within_7")
    if not (np.abs(w) == 1).all(): bad.append("w_one_or_minus_one")
    a = th.reshape(N, 8, 16, D); b = gap.reshape(N, 8, 16, D)
    if (a != a[:, :, :1]).any() or (th < -4096).any() or (th > 4096).any(): bad.append("th")
    if (b != b[:, :, :1]).any() or (gap < 1).any() or (gap > H).any(): bad.append("gap")
    if bad: return bad
    cnt = run(x, v, w, th, gap)[1]
    if cnt.min() < H or cnt.max() > CAP: bad.append("numbers_kept")
    return bad
def reference(x, v, w, th, gap):
    z, cnt = run(x, v, w, th, gap)
    return {"y": z.reshape(N, 128, S).astype(np.float32)}

@@ -1,0 +1,504 @@
+from concourse.bass import DstId, RemoteDMATransfer
+from concourse.mybir import AluOpType, ActivationFunctionType
+
+OP = AluOpType
+AF = ActivationFunctionType
+CAP, HALO, OFS = 2048, 64, 192.0
+XW = HALO + CAP
+V1, Z1, V2, Z2, Z3, BIGW = 4096, 6144, 8192, 10240, 12288, 14336
+DWW, RMW = CAP + 256, 576
+PARTS = [(0, 512), (512, 1024), (1024, 1536), (1536, 1920), (1920, 2048)]
+CUT = 1728
+
+_W = {"bfloat16": {"big": BIGW, "gb": CAP, "gc": CAP, "u": CAP, "cb": CAP, "dc": CAP, "dsb": 256, "mrow": 256,
+                   "e": 144, "bd": 128, "idn": 128, "idk": 128, "idb": 128, "ltf": 128, "lt": 128, "s15": 128, "el1": 144, "el2": 144,
+                   "chi": 16, "clo": 16, "ones": 512, "vb": 3, "cf": 128},
+      "float32": {"yb": 4096, "jrow": 144, "jg": 128, "ir": 256, "iw": 256, "own0": 256, "own1": 128, "m16": 16, "g8": 8, "gm": 8,
+                  "cc": 64, "of1": 16, "of2": 16, "st": 256, "qk": 4, "lcf": 128},
+      "int32": {"ip": 1, "gi": 1, "ki": 1, "thi": 3, "gpi": 3}, "uint16": {}}
+for _t in range(3):
+    for _n, _k, _d in (("xc", XW + HALO, "bfloat16"), ("fl", 2 * HALO, "bfloat16"), ("dw", DWW, "bfloat16"), ("rm", RMW, "bfloat16"),
+                       ("sv", 144, "bfloat16"), ("pen", 128, "bfloat16"), ("iwd", 128, "float32"),
+                       ("lb", 128, "uint16"), ("lc", 128, "uint16"), ("lst", 8, "uint16"), ("fll", 8, "uint16"),
+                       ("off", 16, "uint16"), ("la", 32, "uint16"), ("lm", 32, "uint16"), ("ll", 64, "uint16"),
+                       ("slot", 128 if _t else 256, "uint16")):
+        _W[_d]["%s%d" % (_n, _t)] = _k
+SCRATCH = {n: ("sbuf", [128, k], d) for d, a in _W.items() for n, k in a.items()}
+SCRATCH["wb"] = ("sbuf", [128, 9, 16], "bfloat16")
+SCRATCH["wbd"] = ("sbuf", [128, 9, 128], "bfloat16")
+BANKS = ["b%d" % i for i in range(8)]
+for _b in BANKS:
+    SCRATCH[_b] = ("psum", [128, 512], "float32")
+SEMAPHORES = (["cv", "ca", "cp", "cg", "dv", "dt", "dg", "dwt", "sent"] + ["dx%d" % i for i in range(4)]
+              + ["dy%d" % i for i in range(16)] + ["al%d" % i for i in range(3)] + ["ar%d" % i for i in range(3)])
+PF, GF, KF, G15, K15, ND, SC, BI, BMIN, WL1, WL2, KLO = range(12)
+TH, GAP, G16, VF, KC, KR = 12, 15, 21, 22, 28, 29
+
+
+def tracker(g, T):
+    queues = {"v": g.vector, "a": g.scalar, "p": g.tensor, "g": g, "s": g.sync}
+    count, clock, order, recs, waited = {}, {}, {}, {}, {}
+    known = {e: {} for e in queues}
+    serial = [0]
+
+    def wait(eng, key, n):
+        if known[eng].get(key, 0) >= n:
+            return
+        queues[eng].wait_ge(T.sem[key], n)
+        waited[key] = max(waited.get(key, 0), n)
+        for k2, n2 in clock.get((key, n), {}).items():
+            known[eng][k2] = max(known[eng].get(k2, 0), n2)
+        known[eng][key] = n
+
+    def settle(eng, reads, writes):
+        need = {}
+        for kind, accs in (("r", reads), ("w", writes)):
+            for b, lo, hi in accs:
+                ps = b in BANKS
+                for rk, rlo, rhi, who, key, n in recs.get(b, ()):
+                    over = rlo < hi and lo < rhi
+                    if who == eng:
+                        if eng == "p" or not over or rk == kind == "r":
+                            continue
+                    elif not ps and (not over or rk == kind == "r"):
+                        continue
+                    need[key] = max(need.get(key, 0), n)
+        for key in sorted(need, key=lambda k: -order[(k, need[k])]):
+            wait(eng, key, need[key])
+
+    def note(who, key, n, reads, writes):
+        serial[0] += 1
+        order[(key, n)] = serial[0]
+        for kind, accs in (("r", reads), ("w", writes)):
+            for b, lo, hi in accs:
+                recs.setdefault(b, []).append((kind, lo, hi, who, key, n))
+
+    def emit(eng, fn, reads, writes, dma=None):
+        settle(eng, reads, writes)
+        key, step = (dma, 16) if dma else ("c" + eng, 1)
+        n = count.get(key, 0) + step
+        fn().then_inc(T.sem[key], step)
+        count[key] = n
+        clock[(key, n)] = dict(known[eng])
+        note("dma " + dma if dma else eng, key, n, reads, writes)
+
+    def remote(reads, key, n, fn):
+        settle("g", reads, [])
+        fn()
+        count[key] = count.get(key, 0) + n
+        note("net " + key, key, count[key], reads, [])
+
+    def landing(key, n, writes):
+        count[key] = n
+        note("net " + key, key, n, [], writes)
+
+    def finish():
+        for key in sorted(count):
+            if waited.get(key, 0) < count[key]:
+                wait("s", key, count[key])
+
+    return {"emit": emit, "remote": remote, "landing": landing, "finish": finish}
+
+
+def rank_program(g, core, T, topo):
+    rank = T.rank_of(core)
+    if rank is None:
+        return
+    tr = tracker(g, T)
+    emit = tr["emit"]
+    nranks = len(T.cores)
+
+    def S(name, lo, hi, step=1):
+        if step == 1:
+            return T[name][:, lo:hi], [(name, lo, hi)]
+        return T[name][:, lo:hi:step], [(name, lo, hi)]
+
+    def W(name, lo, hi, lname, l0, l1):
+        return T[name][:, lo:hi].indirect(T[lname][:, l0:l1]), [(name, lo, hi), (lname, l0, l1)]
+
+    def C(col):
+        return S("cc", col, col + 1)
+
+    def split(x):
+        return (x[0], x[1]) if isinstance(x, tuple) else (x, [])
+
+    def ts(out, in0, s1, s2, op0, op1=None):
+        (a1, r1), (a2, r2) = split(s1), split(s2)
+        if op1 is None:
+            emit("v", lambda: g.vector.tensor_scalar(out[0], in0[0], a1, None, op0), in0[1] + r1, out[1])
+        else:
+            emit("v", lambda: g.vector.tensor_scalar(out[0], in0[0], a1, a2, op0, op1), in0[1] + r1 + r2, out[1])
+
+    def tt(out, in0, in1, op):
+        emit("v", lambda: g.vector.tensor_tensor(out[0], in0[0], in1[0], op), in0[1] + in1[1], out[1])
+
+    def vcopy(out, in_):
+        emit("v", lambda: g.vector.tensor_copy(out[0], in_[0]), in_[1], out[1])
+
+    def vscatter(win, in_):
+        emit("v", lambda: g.vector.tensor_copy(win[0], in_[0]), in_[1] + win[1][1:], win[1][:1])
+
+    def vfill(out, c):
+        emit("v", lambda: g.vector.memset(out[0], c), [], out[1])
+
+    def scan(out, d0, d1, init, op0, op1):
+        ai, ri = split(init)
+        emit("v", lambda: g.vector.tensor_tensor_scan(out[0], d0[0], d1[0], ai, op0, op1), d0[1] + d1[1] + ri, out[1])
+
+    def act(out, in_, func, bias=0.0, scale=1.0):
+        (ab, rb), (asc, rs) = split(bias), split(scale)
+        emit("a", lambda: g.scalar.activation(out[0], in_[0], func, bias=ab, scale=asc), in_[1] + rb + rs, out[1])
+
+    def mms(items):
+        def go():
+            last = None
+            for o, l, r, a, b in items:
+                last = g.tensor.matmul(o[0], l[0], r[0], a, b)
+            return last
+        emit("p", go, sorted({a for i in items for a in i[1][1] + i[2][1]}), sorted({a for i in items for a in i[0][1]}))
+
+    def iota(name, lo, hi, pattern, base, cm):
+        if name == "ip":
+            emit("g", lambda: g.iota(T[name][:, lo:hi], pattern, base, cm), [], [(name, lo, hi)])
+        else:
+            emit("g", lambda: g.iota(T[name][:, lo:hi], pattern, base, cm, allow_small_or_imprecise_dtypes=True), [], [(name, lo, hi)])
+
+    def gfill(name, lo, hi, value):
+        iota(name, lo, hi, [[0, hi - lo]], value, 0)
+
+    def load(eng, sem, out, src):
+        q = g.sync if eng == "s" else g.scalar
+        emit(eng, lambda: q.dma_start(out[0], src), [], out[1], dma=sem)
+
+    def win(name, k):
+        return S(name, 15 - k, 143 - k)
+
+    def wrap(out, lhs, name, lo, hi):
+        mms([(out, win(lhs, k), S(name, lo + k, hi, 16), k == 0, k == 15) for k in range(16)])
+
+    def tap(t, j):
+        i = 3 * t + j
+        return T.wbd[:, i, :], [("wbd", i, i + 1)]
+
+    load("a", "dv", S("vb", 0, 3), T.v[:])
+    for c in range(4):
+        load("s", "dx%d" % c, S("big", 1024 * c, 1024 * c + 1024), T.x[:, 1024 * c:1024 * c + 1024])
+    load("a", "dt", S("thi", 0, 3), T.th[:])
+    load("a", "dg", S("gpi", 0, 3), T.gap[:])
+    load("a", "dwt", (T.wb[:, :, :], [("wb", 0, 9)]), T.w[:])
+
+    iota("ip", 0, 1, [[0, 1]], 0, 1)
+    iota("jrow", 0, 144, [[1, 144]], 0, 0)
+    iota("jg", 0, 128, [[1, 8], [0, 16]], 0, 0)
+    iota("ir", 0, 256, [[16, 256]], 0, 1)
+    iota("m16", 0, 16, [[16, 16]], 0, 0)
+    iota("mrow", 0, 256, [[1, 256]], 0, 0)
+    iota("g8", 0, 8, [[1, 8]], 0, 0)
+    for t in range(3):
+        gfill("rm%d" % t, 0, 16, 0)
+    gfill("rm0", 288, 304, 0)
+    gfill("dw0", 1024, CAP, 0)
+    for t in range(3):
+        if rank == 0:
+            gfill("xc%d" % t, 0, HALO, 0)
+        if rank == nranks - 1:
+            gfill("xc%d" % t, XW, XW + HALO, 0)
+    gfill("ones", 0, 512, 1)
+    gfill("dw1", 0, CAP, 0)
+    ts(S("gi", 0, 1), S("ip", 0, 1), 4, None, OP.logical_shift_right)
+    ts(S("ki", 0, 1), S("ip", 0, 1), 15, None, OP.bitwise_and)
+    vcopy(C(PF), S("ip", 0, 1))
+    vcopy(C(GF), S("gi", 0, 1))
+    vcopy(C(KF), S("ki", 0, 1))
+    ts(C(G15), C(GF), 16.0, 15.0, OP.mult, OP.add)
+    ts(C(K15), C(KF), 15.0, None, OP.is_equal)
+    ts(S("e", 0, 144), S("jrow", 0, 144), C(G15), None, OP.is_equal)
+    ts(S("sv0", 0, 144), S("e", 0, 144), S("vb", 0, 1), None, OP.mult)
+    for col, sc, bi in ((ND, 1.0, -1.0), (SC, 2.0, -1.0), (BI, -1.0, 1.0), (BMIN, 255.0, 1.0), (WL1, 15.0, 1.0), (WL2, 17.0, -1.0)):
+        act(C(col), C(K15), AF.Identity, bias=bi, scale=sc)
+    act(C(G16), C(GF), AF.Copy, scale=-16.0)
+    act(C(KLO), C(KF), AF.Copy, scale=-1.0 / 8192)
+    ts(S("bd", 0, 128), S("jg", 0, 128), C(GF), None, OP.is_equal)
+    ts(S("ltf", 0, 128), S("jrow", 0, 128), C(PF), None, OP.is_ge)
+    ts(S("idn", 0, 128), S("jrow", 0, 128), C(PF), None, OP.is_equal)
+    tt(S("ltf", 0, 128), S("ltf", 0, 128), S("bd", 0, 128), OP.mult)
+    ts(S("s15", 0, 128), S("idn", 0, 128), C(K15), None, OP.mult)
+    tt(S("lt", 0, 128), S("ltf", 0, 128), S("e", 0, 128), OP.subtract)
+    vcopy(S("cc", TH, TH + 3), S("thi", 0, 3))
+    vfill(S("dw0", 0, 1024), 0.0)
+    vcopy(S("cc", GAP, GAP + 3), S("gpi", 0, 3))
+    vcopy(S("cc", VF, VF + 3), S("vb", 0, 3))
+    ts(S("iw", 0, 256), S("ir", 0, 256), C(G16), None, OP.add)
+    ts(S("chi", 0, 16), S("m16", 0, 16), 2048.0, -1.0 / 8192, OP.add, OP.mult)
+    ts(S("clo", 0, 16), S("m16", 0, 16), 0.0, C(KLO), OP.mult, OP.add)
+    for lo in (0, 1024):
+        act(S("dc", lo, lo + 1024), S("big", 0, 1024), AF.Identity, bias=C(ND), scale=0.0)
+    for t in (1, 2):
+        act(S("sv%d" % t, 0, 144), S("e", 0, 144), AF.Copy, scale=C(VF + t))
+    ts(S("gm", 0, 8), S("g8", 0, 8), C(GF), 0.125, OP.is_equal, OP.mult)
+    act(S("iwd0", 0, 128), S("iw", 0, 128), AF.Identity, bias=C(GAP))
+    act(S("qk", 0, 4), S("iw", 0, 4), AF.Identity, bias=-64.0)
+    act(S("el1", 0, 144), S("e", 0, 144), AF.Copy, scale=C(WL1))
+    act(S("el2", 0, 144), S("e", 0, 144), AF.Copy, scale=C(WL2))
+    base = [4096 - 1 - 8192, 2048 - 1 - 8192]
+
+    def tap_matrices(first, last):
+        for i in range(first, last):
+            emit("a", lambda: g.scalar.activation(T.wbd[:, :, 16 * i:16 * i + 16], T.wb[:, :, :], AF.Copy, scale=T.gm[:, i:i + 1]),
+                 [("wb", 0, 9), ("gm", i, i + 1)], [("wbd", 0, 9)] if i == 7 else [])
+
+    def later_constants():
+        for i, n in ((0, 256), (1, 128)):
+            act(S("own%d" % i, 0, n), S("iw", 0, n), AF.Identity, bias=float(-base[i]))
+        for t in (1, 2):
+            act(S("iwd%d" % t, 0, 128), S("iw", 0, 128), AF.Identity, bias=C(GAP + t))
+            act(C(TH + t), S("b3", 300 + t, 301 + t), AF.Identity, bias=C(TH + t), scale=OFS)
+
+    def shift_lists(t):
+        ts(S("lst%d" % t, 0, 4), S("iw", 0, 4), C(GAP + t), 64.0, OP.subtract, OP.add)
+        ts(S("lb%d" % t, 4, 128), S("iw", 4, 128), C(GAP + t), None, OP.subtract)
+
+    def slots_a(t):
+        n = 128 if t else 256
+        tt(S("st", 0, n), S("own%d" % (t > 0), 0, n), S("b3", 16, 16 + n), OP.max)
+
+    def slots_b(t):
+        n = 128 if t else 256
+        ts(S("slot%d" % t, 0, n), S("st", 0, n), float(base[t > 0]), None, OP.add)
+
+    zoff = [Z1, Z2, Z3]
+
+    def send(t):
+        fl, x = "fl%d" % t, "xc%d" % t
+        out = []
+        if rank > 0:
+            out.append((rank - 1, S(fl, 0, HALO), T[x][:, XW:XW + HALO], "ar%d" % t))
+        if rank < nranks - 1:
+            out.append((rank + 1, S(fl, HALO, 2 * HALO), T[x][:, 0:HALO], "al%d" % t))
+        reads = [a for o in out for a in o[1][1]]
+        if len(out) == 1:
+            dst = T.cores[out[0][0]]
+            a = topo.addr(dst)
+            tr["remote"](reads, "sent", len(topo.engines(core, dst)), lambda: g.remote_dma(
+                out_ap=out[0][2], in_ap=out[0][1][0], remote_sem=T.sem[out[0][3]], local_sem=T.sem.sent,
+                pid=a[1], routing_id=a[0], dma_engine_mask=topo.mask(core, dst)))
+            return
+        trs, used = [], 0
+        for i, o in enumerate(out):
+            dst = T.cores[o[0]]
+            a = topo.addr(dst)
+            en = topo.engines(core, dst)
+            half = len(en) // 2
+            mine = en[:half] if i == 0 else en[half:]
+            used += len(mine)
+            trs.append(RemoteDMATransfer(dst_ids=[DstId(rid=a[0], pnc=a[1])], dma_engine_mask=sum(1 << k for k in mine),
+                                         remote_sem=T.sem[o[3]], src=o[1][0], dst=o[2]))
+        tr["remote"](reads, "sent", used, lambda: g.remote_dma_fused(trs, local_sem=T.sem.sent))
+
+    for t in range(3):
+        for peer, key, lo in ((rank - 1, "al%d" % t, 0), (rank + 1, "ar%d" % t, XW)):
+            if 0 <= peer < nranks:
+                en = len(topo.engines(T.cores[peer], core))
+                tr["landing"](key, en if peer in (0, nranks - 1) else en // 2, [("xc%d" % t, lo, lo + HALO)])
+
+    def scores(t, half):
+        ob = S("b0", 0, 64) if half == 0 else S("b2", 0, 64)
+        c0, s0 = 64 * half, zoff[t - 1] + 1024 * half
+        mms([(ob, S("idn", 0, 128), S("pen%d" % t, c0, c0 + 64), True, False)]
+            + [(ob, win("sv%d" % t, k), S("big", s0 + k, s0 + 1024, 16), False, k == 15) for k in range(16)])
+
+    def back(eng, level, lo, hi):
+        src, top = ((0, V1), (Z1, V2), (Z2, Z3))[level]
+        i = W("big", src, top + min(hi, CAP), "slot%d" % level, lo // 16, hi // 16)
+        o = S("yb", lo, hi) if level == 0 else S("big", (0, V1, V2)[level] + lo, (0, V1, V2)[level] + hi)
+        if eng == "a":
+            act(o, i, AF.Copy) if level != 1 else act(o, i, AF.Identity, bias=-OFS)
+        elif level != 1:
+            vcopy(o, i)
+        else:
+            ts(o, i, -OFS, None, OP.add)
+
+    def store(lo, hi):
+        emit("s", lambda: g.sync.dma_start(T.y[:, lo:hi], T.yb[:, lo:hi]), [("yb", lo, hi)], [], dma="dy%d" % (lo // 256))
+
+    for t in range(3):
+        rm, dw, xc, lst, fl, sv = ["%s%d" % (n, t) for n in ("rm", "dw", "xc", "lst", "fl", "sv")]
+        space = (0, 4096) if t == 0 else (zoff[t - 1], zoff[t - 1] + CAP)
+        z = zoff[t]
+        P0 = (16, 304) if t == 0 else (16,)
+        last = len(P0) - 1
+
+        def mark(p):
+            m0, r0, c0, w0, o = P0[p], P0[p] + 128, 128 * p, 8 * p, 32 * p
+            mms([(S("b1", c0, c0 + 128), S("lt", 0, 128), S(rm, m0, r0), True, False),
+                 (S("b1", c0, c0 + 128), S("s15", 0, 128), S("mrow", c0, c0 + 128), False, True)])
+            scan(S(rm, r0, r0 + 129), S(rm, m0 - 1, r0), S(rm, m0 - 1, r0), S(rm, P0[0] + 256, P0[0] + 257) if p else 0.0, OP.add, OP.max)
+            act(S("dsb", c0, c0 + 128), S("b1", c0, c0 + 128), AF.Copy)
+            if p == last:
+                mms([(S("b3", 0, 1), S("bd", 0, 128), S(rm, r0 + 128, r0 + 129), True, True)])
+            b2, b2m = S("b2", o, o + 16), S("b2", o, o + 8)
+            rhs = [(win("e", k), S(rm, m0 + k, m0 + 256, 16)) for k in range(16)]
+            mms([(b2, rhs[0][0], rhs[0][1], True, False),
+                 (b2m, S("idn", 0, 128), S("chi", w0, w0 + 8), False, False), (b2m, S("idn", 0, 128), S("clo", w0, w0 + 8), False, False)]
+                + [(b2, rhs[k][0], rhs[k][1], False, k == 15) for k in range(1, 16)])
+
+        def offsets(p, fill1=None, fill2=None):
+            w0, o = 8 * p, 32 * p
+            ts(S("of1", w0, w0 + 8), S("b2", o, o + 8), -8192.0, None, OP.mult)
+            if fill1:
+                fill1()
+            tt(S("of2", w0, w0 + 8), S("of1", w0, w0 + 8), S("b2", o + 8, o + 16), OP.max)
+            if fill2:
+                fill2()
+            vcopy(S("off%d" % t, w0, w0 + 8), S("of2", w0, w0 + 8))
+
+        def scatter(p):
+            vscatter(W(dw, 0, DWW, "off%d" % t, 8 * p, 8 * p + 8), S("dsb", 128 * p, 128 * p + 128))
+
+        def pick(eng, out, lname, l0, l1):
+            i = W("big", *space, lname, l0, l1)
+            if eng == "a":
+                act(out, i, AF.Copy) if t == 0 else act(out, i, AF.Identity, bias=-OFS)
+            else:
+                vcopy(out, i) if t == 0 else ts(out, i, -OFS, None, OP.add)
+
+        def left(eng, lo, hi):
+            o, i = S("gb", lo, hi), W(xc, HALO, HALO + hi, "lb%d" % t, lo // 16, hi // 16)
+            act(o, i, AF.Copy) if eng == "a" else vcopy(o, i)
+
+        def right(eng, lo, hi):
+            o, i = S("gc", lo, hi), W(xc, HALO, XW + HALO, "lc%d" % t, lo // 16, hi // 16)
+            act(o, i, AF.Copy) if eng == "a" else vcopy(o, i)
+
+        def bank(c):
+            return S(("b4", "b5", "b6", "b7", "b1")[c], 0, PARTS[c][1] - PARTS[c][0])
+
+        def offset(c):
+            mms([(bank(c), S("idb", 0, 128), S("ones", 0, PARTS[c][1] - PARTS[c][0]), True, False)])
+
+        def mix(c, j):
+            lo, hi = PARTS[c]
+            mms([(bank(c), tap(t, j), S(*((xc, HALO + lo, HALO + hi), ("gb", lo, hi), ("gc", lo, hi))[j]), False, j == 2)])
+
+        def near(c):
+            lo, hi = PARTS[c]
+            ts(S("big", z + lo, z + hi), bank(c), OFS - 15.0, OFS + 15.0, OP.max, OP.min)
+
+        if t == 0:
+            for c in range(4):
+                wrap(S("b0" if c < 2 else "b3", 64 * (c % 2), 64 * (c % 2) + 64), sv, "big", 1024 * c, 1024 * c + 1024)
+                if c == 1:
+                    ts(S(rm, 16, 144), S("b0", 0, 128), C(TH), None, OP.is_ge)
+                if c == 2:
+                    tap_matrices(0, 2)
+                    mark(0)
+            shift_lists(0)
+            for name, c in (("idk", 8192.0), ("idb", OFS)):
+                ts(S(name, 0, 128), S("idn", 0, 128), c, None, OP.mult)
+            offsets(0)
+            ts(S(rm, 304, 432), S("b3", 0, 128), C(TH), None, OP.is_ge)
+        else:
+            scores(t, 1)
+            shift_lists(t)
+            slots_a(t - 1)
+            ts(S(rm, 16, 80), S("b0", 0, 64), C(TH + t), None, OP.is_ge)
+            ts(S(rm, 80, 144), S("b2", 0, 64), C(TH + t), None, OP.is_ge)
+        mark(last)
+        if t == 0:
+            scatter(0)
+        else:
+            slots_b(t - 1)
+        act(C(KR), S("b3", 0, 1), AF.Copy)
+        act(C(KC), S("b3", 0, 1), AF.Copy, bias=float(XW - HALO), scale=-1.0)
+        lcsel = S("b0", 256, 384)
+        offsets(last, lambda: ts(lcsel, S("iwd%d" % t, 0, 128), C(KR), C(KC), OP.is_ge, OP.mult),
+                lambda: ts(S(lst, 4, 8), S("qk", 0, 4), C(KR), None, OP.add))
+        scatter(last)
+        for p in range(last + 1):
+            cum, m0 = S("b3", 16 + 128 * p, 144 + 128 * p), P0[p]
+            mms([(cum, S("bd", 0, 128), S(rm, m0 + 128, m0 + 256), True, False), (cum, S("ltf", 0, 128), S(rm, m0, m0 + 128), False, False),
+                 (cum, S("idk", 0, 128), S(rm, m0, m0 + 128), False, True)])
+        if t == 0:
+            tap_matrices(2, 8)
+            mms([(S("b3", 300, 303), S("bd", 0, 128), S("vb", 0, 3), True, True)])
+        u0 = 0.0
+        for lo, hi in ((0, 512), (512, 1024), (1024, 2048)):
+            scan(S("u", lo, hi), S("dc", lo, hi), S(dw, lo, hi), u0, OP.add, OP.max)
+            if lo < 1024:
+                act(S("cb", lo, hi), S("u", lo, hi), AF.Relu, bias=C(BI), scale=C(SC))
+            if lo == 0:
+                tt(S("lcf", 0, 128), S("iwd%d" % t, 0, 128), lcsel, OP.add)
+            if lo == 512:
+                ts(S("cf", 0, 64), S("u", 0, 64), C(BMIN), None, OP.min)
+            if lo == 1024:
+                ts(S("lc%d" % t, 0, 128), S("lcf", 0, 128), float(CAP + HALO - 1), None, OP.min)
+            u0 = S("u", hi - 1, hi)
+        ts(S("cf", 64, 128), W("u", 0, CAP, lst, 4, 8), C(BMIN), None, OP.min)
+        for c in range(3):
+            offset(c)
+        wrap(S("b1", 0, 32), "el1", "cb", 0, 512)
+        wrap(S("b2", 0, 8), "el2", "cf", 0, 128)
+        vcopy(S("la%d" % t, 0, 32), S("b1", 0, 32))
+        pick("a", S(xc, 64, 576), "la%d" % t, 0, 32)
+        ts(S("cb", 1024, 2048), S("u", 1024, 2048), C(BMIN), None, OP.min)
+        ts(S("fll%d" % t, 0, 8), S("b2", 0, 8), 15.0, None, OP.add)
+        pick("v", S(fl, 0, 128), "fll%d" % t, 0, 8)
+        send(t)
+        wrap(S("b1", 0, 32), "el1", "cb", 512, 1024)
+        wrap(S("b0", 0, 64), "el2", "cb", 1024, 2048)
+        vcopy(S("lm%d" % t, 0, 32), S("b1", 0, 32))
+        pick("a", S(xc, 576, 1088), "lm%d" % t, 0, 32)
+        ts(S("ll%d" % t, 0, 64), S("b0", 0, 64), 15.0, None, OP.add)
+        pick("v", S(xc, 1088, 64 + CUT), "ll%d" % t, 0, CUT // 16 - 64)
+        pick("a", S(xc, 64 + CUT, 2112), "ll%d" % t, CUT // 16 - 64, 64)
+        offset(3)
+        offset(4)
+        left("a", 64, 512)
+        left("v", 1024, 1536)
+        left("a", 512, 1024)
+        left("v", 1536, 2048)
+        for c in range(5):
+            mix(c, 0)
+        vcopy(S("gb", 0, 64), W(xc, 0, HALO + 64, lst, 0, 4))
+        right("a", 0, 512)
+        for c in (2, 1, 3, 4, 0):
+            mix(c, 1)
+        right("v", 1536, 1920)
+        mix(0, 2)
+        right("a", 512, 1024)
+        mix(3, 2)
+        right("a", 1024, 1536)
+        mix(1, 2)
+        if t < 2:
+            ts(S("pen%d" % (t + 1), 0, 128), S("iw", 0, 128), C(KR), -32768.0, OP.is_ge, OP.mult)
+        else:
+            slots_a(2)
+        right("a", 1920, 2048)
+        if t == 0:
+            later_constants()
+        mix(2, 2)
+        mix(4, 2)
+        if t == 2:
+            slots_b(2)
+        near(0)
+        if t == 2:
+            back("a", 2, 0, 512)
+        near(3)
+        near(1)
+        if t == 2:
+            back("a", 1, 0, 512)
+        if t < 2:
+            scores(t + 1, 0)
+        near(2)
+        near(4)
+        if t == 0:
+            gfill("dw2", 0, CAP, 0)
+
+    for level, c in ((2, 1), (0, 0), (1, 1), (2, 2), (0, 1), (1, 2), (2, 3), (0, 2), (1, 3), (0, 3), (0, 4), (0, 5), (0, 6), (0, 7)):
+        for lo, hi in ((512 * c, 512 * c + 512),) if (level, c) != (0, 7) else ((3584, 3840), (3840, 4096)):
+            mid = (lo + hi) // 2
+            back("a", level, lo, mid)
+            back("v", level, mid, hi)
+            if level == 0:
+                store(lo, hi)
+    tr["finish"]()

@@ -3,36 +3,48 @@ from concourse.mybir import AluOpType, ActivationFunctionType
 
 OP = AluOpType
 AF = ActivationFunctionType
-CAP, HALO, OFS = 2048, 64, 192.0
-XW = HALO + CAP
+CAP, HALO, OFS, BIG = 2048, 64, 192.0, 32768.0
+X0 = 2 * HALO
+XZ = X0 + CAP
 V1, Z1, V2, Z2, Z3, BIGW = 4096, 6144, 8192, 10240, 12288, 14336
-DWW, RMW = CAP + 256, 576
+TAIL, M0 = 80, 112
+L0 = (M0 - 16) // 16
+RMW = 576
 PARTS = [(0, 512), (512, 1024), (1024, 1536), (1536, 1920), (1920, 2048)]
-CUT = 1728
+MIXB = ("b4", "b5", "b6", "b7", "b3")
+_LIST = "o0123 tail u0 utail u1 W01 L0 lc1 pa0-64 lastv send pa64-640 lc2 lc3 L1 pa640-1280 pv1280-2048 counts "
+PAR = {"cuts": [640], "fill": 1024,
+       "mid": _LIST + """pen A0123 o4 A4 la0-512 lv1024-1536 la512-1024 lv1536-2048 B0213 edgev E0 ra0-256 rv256-512 C0
+           ra512-1024 rv1024-1408 E1 C1 n0 B4 E234 ra1408-1536 C2 ra1536-1920 n1 s0 C3 ra1920-2048 n2 base s1 C4 n3 preset s2 n4 s3 S4""",
+       "end": _LIST + """o4 la64-512 slots lv1024-1536 la512-1024 slots2 lv1536-2048 A01234 edgev B21340
+           rx0-512 C0 ra512-1024 rv1024-1536 C12 n0 ra1536-1920 C3 n1 ra1920-2048 C4 2a0-512 n2 n3 1a0-512 n4
+           2v512-1024 0a0-512 y.0-512 2v1024-1536 1a512-1024 2v1536-2048 0a512-1024 y.512-1024 1v1024-1536 1a1536-2048
+           0v1024-1536 y.1024-1536 0a1536-2048 y.1536-2048 0x2048-2560 y.2048-2560 0x2560-3072 y.2560-3072 0x3072-3584 y.3072-3584
+           0x3584-3840 y.3584-3840 0x3840-4096 y.3840-4096"""}
 
-_W = {"bfloat16": {"big": BIGW, "gb": CAP, "gc": CAP, "u": CAP, "cb": CAP, "dc": CAP, "dsb": 256, "mrow": 256,
-                   "e": 144, "bd": 128, "idn": 128, "idk": 128, "idb": 128, "ltf": 128, "lt": 128, "s15": 128, "el1": 144, "el2": 144,
-                   "chi": 16, "clo": 16, "ones": 512, "vb": 3, "cf": 128},
-      "float32": {"yb": 4096, "jrow": 144, "jg": 128, "ir": 256, "iw": 256, "own0": 256, "own1": 128, "m16": 16, "g8": 8, "gm": 8,
-                  "cc": 64, "of1": 16, "of2": 16, "st": 256, "qk": 4, "lcf": 128},
-      "int32": {"ip": 1, "gi": 1, "ki": 1, "thi": 3, "gpi": 3}, "uint16": {}}
+_W = {"bfloat16": {"big": BIGW, "gb": CAP, "gc": CAP, "ge": HALO, "u": M0 + CAP, "dc": 1408, "dsb": 256, "jrow": 256, "jg": 128, "jk": 128,
+                   "e": 144, "bd": 128, "nbd": 128, "idn": 128, "idk": 128, "idb": 128, "idm": 128, "ltf": 128, "lt": 128, "s15": 128,
+                   "own0e": 144, "own1e": 144, "nxt0e": 144, "nxt1e": 144, "two0e": 144, "two1e": 144,
+                   "cp": 256, "rs": 256, "ones": 512, "vb": 3, "pen": 128},
+      "float32": {"yb": 4096, "iw": 128, "iwp": 128, "iwl": 128, "iwe": 4, "own0": 256, "own1": 128,
+                  "gm": 8, "cc": 64, "pk": 256, "st": 256, "qk": 5, "lcf": 128},
+      "int32": {"ip": 1, "gi": 1, "ki": 1, "ei": 1, "thi": 3, "gpi": 3}, "uint16": {}}
 for _t in range(3):
-    for _n, _k, _d in (("xc", XW + HALO, "bfloat16"), ("fl", 2 * HALO, "bfloat16"), ("dw", DWW, "bfloat16"), ("rm", RMW, "bfloat16"),
-                       ("sv", 144, "bfloat16"), ("pen", 128, "bfloat16"), ("iwd", 128, "float32"),
-                       ("lb", 128, "uint16"), ("lc", 128, "uint16"), ("lst", 8, "uint16"), ("fll", 8, "uint16"),
-                       ("off", 16, "uint16"), ("la", 32, "uint16"), ("lm", 32, "uint16"), ("ll", 64, "uint16"),
-                       ("slot", 128 if _t else 256, "uint16")):
+    for _n, _k, _d in (("xc", XZ + 16, "bfloat16"), ("fl", HALO, "bfloat16"), ("dw", M0 + CAP + 128, "bfloat16"), ("rm", RMW, "bfloat16"),
+                       ("sv", 144, "bfloat16"), ("iwd", 128, "float32"),
+                       ("lb", 128, "uint16"), ("lc", 128, "uint16"), ("lst", 4, "uint16"), ("lse", 6, "uint16"),
+                       ("off", 16, "uint16"), ("ls", L0 + 128, "uint16"), ("slot", 128 if _t else 256, "uint16")):
         _W[_d]["%s%d" % (_n, _t)] = _k
 SCRATCH = {n: ("sbuf", [128, k], d) for d, a in _W.items() for n, k in a.items()}
 SCRATCH["wb"] = ("sbuf", [128, 9, 16], "bfloat16")
 SCRATCH["wbd"] = ("sbuf", [128, 9, 128], "bfloat16")
 BANKS = ["b%d" % i for i in range(8)]
 for _b in BANKS:
-    SCRATCH[_b] = ("psum", [128, 512], "float32")
+    SCRATCH[_b] = ("psum", [128, 4, 128] if _b in MIXB[:4] else [128, 512], "float32")
 SEMAPHORES = (["cv", "ca", "cp", "cg", "dv", "dt", "dg", "dwt", "sent"] + ["dx%d" % i for i in range(4)]
               + ["dy%d" % i for i in range(16)] + ["al%d" % i for i in range(3)] + ["ar%d" % i for i in range(3)])
-PF, GF, KF, G15, K15, ND, SC, BI, BMIN, WL1, WL2, KLO = range(12)
-TH, GAP, G16, VF, KC, KR = 12, 15, 21, 22, 28, 29
+PF, GF, KF, G15, K15, K00, K16, ND, RB, W0, R4, E0, OW0, OW1, NX0, NX1, OWN0, OWN1, KS, KP = range(20)
+TH, GAP, GPX, VF = 24, 27, 30, 33
 
 
 def tracker(g, T):
@@ -170,11 +182,17 @@ def rank_program(g, core, T, topo):
         q = g.sync if eng == "s" else g.scalar
         emit(eng, lambda: q.dma_start(out[0], src), [], out[1], dma=sem)
 
+    def gather(eng, out, i, add=None):
+        if eng == "a":
+            act(out, i, AF.Copy) if add is None else act(out, i, AF.Identity, bias=add)
+        else:
+            vcopy(out, i) if add is None else ts(out, i, add, None, OP.add)
+
+    def scaled(eng, out, in_, by):
+        act(out, in_, AF.Copy, scale=by) if eng == "a" else ts(out, in_, by, None, OP.mult)
+
     def win(name, k):
         return S(name, 15 - k, 143 - k)
-
-    def wrap(out, lhs, name, lo, hi):
-        mms([(out, win(lhs, k), S(name, lo + k, hi, 16), k == 0, k == 15) for k in range(16)])
 
     def tap(t, j):
         i = 3 * t + j
@@ -187,80 +205,126 @@ def rank_program(g, core, T, topo):
     load("a", "dg", S("gpi", 0, 3), T.gap[:])
     load("a", "dwt", (T.wb[:, :, :], [("wb", 0, 9)]), T.w[:])
 
+    jrow, bd, e, idn = S("jrow", 0, 128), S("bd", 0, 128), S("e", 0, 144), S("idn", 0, 128)
+    dcw = max(b - a for a, b in zip([0] + PAR["cuts"], PAR["cuts"] + [CAP]))
+    base = [4096 - 1 - 8192, 2048 - 1 - 8192]
+    weights = ((1.0, 16.0), (128.0, 1.0))
     iota("ip", 0, 1, [[0, 1]], 0, 1)
     iota("jrow", 0, 144, [[1, 144]], 0, 0)
+    iota("jk", 0, 128, [[0, 8], [1, 16]], 0, 0)
     iota("jg", 0, 128, [[1, 8], [0, 16]], 0, 0)
-    iota("ir", 0, 256, [[16, 256]], 0, 1)
-    iota("m16", 0, 16, [[16, 16]], 0, 0)
-    iota("mrow", 0, 256, [[1, 256]], 0, 0)
-    iota("g8", 0, 8, [[1, 8]], 0, 0)
-    for t in range(3):
-        gfill("rm%d" % t, 0, 16, 0)
-    gfill("rm0", 288, 304, 0)
-    gfill("dw0", 1024, CAP, 0)
+    iota("jrow", 144, 256, [[1, 112]], 144, 0)
+    iota("iwp", 0, 128, [[1, 16], [256, 8]], 0, 0)
+    gfill("dw0", M0 + PAR["fill"], M0 + CAP, 0)
+    gfill("u", TAIL, M0, 0)
+    gfill("ones", 0, 512, 1)
     for t in range(3):
         if rank == 0:
-            gfill("xc%d" % t, 0, HALO, 0)
+            gfill("xc%d" % t, HALO, X0, 0)
         if rank == nranks - 1:
-            gfill("xc%d" % t, XW, XW + HALO, 0)
-    gfill("ones", 0, 512, 1)
-    gfill("dw1", 0, CAP, 0)
+            gfill("xc%d" % t, 0, HALO, 0)
+        if t:
+            gfill("rm%d" % t, 15, 16, 0)
+        if t < 2:
+            gfill("xc%d" % t, XZ, XZ + 16, 0)
+    vfill(S("rs", 0, 256), 0.0)
     ts(S("gi", 0, 1), S("ip", 0, 1), 4, None, OP.logical_shift_right)
     ts(S("ki", 0, 1), S("ip", 0, 1), 15, None, OP.bitwise_and)
-    vcopy(C(PF), S("ip", 0, 1))
+    vfill(S("rs", 0, 256, 32), -2 * BIG)
     vcopy(C(GF), S("gi", 0, 1))
     vcopy(C(KF), S("ki", 0, 1))
+    vcopy(C(PF), S("ip", 0, 1))
     ts(C(G15), C(GF), 16.0, 15.0, OP.mult, OP.add)
     ts(C(K15), C(KF), 15.0, None, OP.is_equal)
-    ts(S("e", 0, 144), S("jrow", 0, 144), C(G15), None, OP.is_equal)
-    ts(S("sv0", 0, 144), S("e", 0, 144), S("vb", 0, 1), None, OP.mult)
-    for col, sc, bi in ((ND, 1.0, -1.0), (SC, 2.0, -1.0), (BI, -1.0, 1.0), (BMIN, 255.0, 1.0), (WL1, 15.0, 1.0), (WL2, 17.0, -1.0)):
-        act(C(col), C(K15), AF.Identity, bias=bi, scale=sc)
-    act(C(G16), C(GF), AF.Copy, scale=-16.0)
-    act(C(KLO), C(KF), AF.Copy, scale=-1.0 / 8192)
-    ts(S("bd", 0, 128), S("jg", 0, 128), C(GF), None, OP.is_equal)
-    ts(S("ltf", 0, 128), S("jrow", 0, 128), C(PF), None, OP.is_ge)
-    ts(S("idn", 0, 128), S("jrow", 0, 128), C(PF), None, OP.is_equal)
-    tt(S("ltf", 0, 128), S("ltf", 0, 128), S("bd", 0, 128), OP.mult)
-    ts(S("s15", 0, 128), S("idn", 0, 128), C(K15), None, OP.mult)
-    tt(S("lt", 0, 128), S("ltf", 0, 128), S("e", 0, 128), OP.subtract)
+    ts(C(K00), C(KF), 0.0, None, OP.is_equal)
+    ts(e, S("jrow", 0, 144), C(G15), None, OP.is_equal)
+    ts(C(RB), C(K15), C(K00), -1.0, OP.add, OP.add)
+    ts(idn, jrow, C(PF), None, OP.is_equal)
+    vfill(S("rm0", 15, 304, 288), 0.0)
+    act(C(W0), C(KF), AF.Copy, bias=15.0, scale=-1.0)
+    act(C(K16), C(KF), AF.Copy, scale=16.0)
+    act(C(ND), C(K00), AF.Identity, bias=C(RB), scale=-256.0)
+    for i, (wp, wb) in enumerate(weights):
+        act(C(OW0 + i), C(K15), AF.Copy, bias=wp, scale=wb - wp)
+        act(C(NX0 + i), C(RB), AF.Copy, scale=wp)
+        act(C(OW0 + i), C(K00), AF.Identity, bias=C(OW0 + i), scale=-2 * wp)
+    ts(S("ltf", 0, 128), S("jk", 0, 128), C(KF), None, OP.is_ge)
+    ts(S("sv0", 0, 144), e, S("vb", 0, 1), None, OP.mult)
+    for i in (0, 1):
+        ts(S("cp", i, 256, 2), S("jk", 0, 128), C(KF), BIG + CAP * i, OP.is_equal, OP.mult)
+    ts(bd, S("jg", 0, 128), C(GF), None, OP.is_equal)
+    ts(S("s15", 0, 128), idn, C(K15), None, OP.mult)
+    tt(S("ltf", 0, 128), S("ltf", 0, 128), bd, OP.mult)
+    act(S("nbd", 0, 128), bd, AF.Copy, scale=-8192.0)
     vcopy(S("cc", TH, TH + 3), S("thi", 0, 3))
-    vfill(S("dw0", 0, 1024), 0.0)
-    vcopy(S("cc", GAP, GAP + 3), S("gpi", 0, 3))
-    vcopy(S("cc", VF, VF + 3), S("vb", 0, 3))
-    ts(S("iw", 0, 256), S("ir", 0, 256), C(G16), None, OP.add)
-    ts(S("chi", 0, 16), S("m16", 0, 16), 2048.0, -1.0 / 8192, OP.add, OP.mult)
-    ts(S("clo", 0, 16), S("m16", 0, 16), 0.0, C(KLO), OP.mult, OP.add)
-    for lo in (0, 1024):
-        act(S("dc", lo, lo + 1024), S("big", 0, 1024), AF.Identity, bias=C(ND), scale=0.0)
-    for t in (1, 2):
-        act(S("sv%d" % t, 0, 144), S("e", 0, 144), AF.Copy, scale=C(VF + t))
-    ts(S("gm", 0, 8), S("g8", 0, 8), C(GF), 0.125, OP.is_equal, OP.mult)
-    act(S("iwd0", 0, 128), S("iw", 0, 128), AF.Identity, bias=C(GAP))
-    act(S("qk", 0, 4), S("iw", 0, 4), AF.Identity, bias=-64.0)
-    act(S("el1", 0, 144), S("e", 0, 144), AF.Copy, scale=C(WL1))
-    act(S("el2", 0, 144), S("e", 0, 144), AF.Copy, scale=C(WL2))
-    base = [4096 - 1 - 8192, 2048 - 1 - 8192]
+    tt(S("lt", 0, 128), S("ltf", 0, 128), S("e", 0, 128), OP.subtract)
+    ts(S("qk", 0, 5), S("jrow", 0, 5), 16.0, C(KF), OP.mult, OP.add)
+    ts(S("lt", 0, 128, 16), S("bd", 0, 128, 16), C(W0), None, OP.mult)
+    act(S("dw0", M0 - 16, M0 + PAR["fill"]), S("big", 0, PAR["fill"] + 16), AF.Copy, scale=0.0)
 
-    def tap_matrices(first, last):
-        for i in range(first, last):
+    def steps_row():
+        act(S("dc", 0, dcw), S("big", 0, dcw), AF.Identity, bias=C(ND), scale=0.0)
+
+    def list_matrices(eng, i):
+        own, nxt, two = ["%s%de" % (n, i) for n in ("own", "nxt", "two")]
+        scaled(eng, S(two, 0, 144), e, C(OW0 + i))
+        scaled(eng, S(nxt, 0, 144), e, C(NX0 + i))
+        scaled(eng, S(own, 0, 144), e, C(OW0 + i))
+        scaled(eng, S(two, 16, 144, 16), S("bd", 0, 128, 16), C(NX0 + i))
+
+    def tap_matrices():
+        for i in range(8):
             emit("a", lambda: g.scalar.activation(T.wbd[:, :, 16 * i:16 * i + 16], T.wb[:, :, :], AF.Copy, scale=T.gm[:, i:i + 1]),
                  [("wb", 0, 9), ("gm", i, i + 1)], [("wbd", 0, 9)] if i == 7 else [])
 
+    def small_columns(part):
+        if part == 0:
+            vcopy(S("cc", GAP, GAP + 3), S("gpi", 0, 3))
+            ts(S("ei", 0, 1), S("ki", 0, 1), 2, None, OP.logical_shift_right)
+            ts(C(R4), C(KF), 4.0, 4096.0, OP.is_lt, OP.mult)
+        else:
+            vcopy(C(E0), S("ei", 0, 1))
+            ts(S("gm", 0, 8), S("jrow", 0, 8), C(GF), 0.125, OP.is_equal, OP.mult)
+            vcopy(S("cc", VF, VF + 3), S("vb", 0, 3))
+
+    def place_rows():
+        act(S("idb", 0, 128), idn, AF.Copy, scale=OFS)
+        act(S("iwp", 0, 128), S("iwp", 0, 128), AF.Identity, bias=C(K16))
+        act(S("cc", GPX, GPX + 3), S("cc", GAP, GAP + 3), AF.Copy, bias=float(X0))
+        act(S("iwl", 0, 128), S("iwp", 0, 128), AF.Copy)
+        right_base(0)
+        act(S("iwl", 0, 128, 8), S("iwp", 0, 128, 8), AF.Identity, bias=C(R4))
+
+    def edge_places():
+        act(C(E0), C(E0), AF.Identity, bias=C(K16), scale=-63.0)
+        act(S("iw", 0, 128), jrow, AF.Identity, bias=C(KF), scale=16.0)
+        act(S("iwe", 0, 4), S("jrow", 0, 4), AF.Identity, bias=C(E0), scale=4.0)
+
     def later_constants():
-        for i, n in ((0, 256), (1, 128)):
-            act(S("own%d" % i, 0, n), S("iw", 0, n), AF.Identity, bias=float(-base[i]))
-        for t in (1, 2):
-            act(S("iwd%d" % t, 0, 128), S("iw", 0, 128), AF.Identity, bias=C(GAP + t))
-            act(C(TH + t), S("b3", 300 + t, 301 + t), AF.Identity, bias=C(TH + t), scale=OFS)
+        for i in (1, 2):
+            act(C(TH + i), S("b2", 400 + i, 401 + i), AF.Identity, bias=C(TH + i), scale=OFS)
+        act(C(OWN0), C(KF), AF.Copy, bias=float(-base[0]))
+        act(C(OWN1), C(KF), AF.Copy, bias=float(-base[1]), scale=128.0)
+        act(S("own0", 0, 256), S("jrow", 0, 256), AF.Identity, bias=C(OWN0), scale=16.0)
+        list_matrices("a", 1)
+        act(S("own1", 0, 128), jrow, AF.Identity, bias=C(OWN1))
+        act(S("sv2", 0, 144), e, AF.Copy, scale=C(VF + 2))
+
+    def right_base(t):
+        act(S("iwd%d" % t, 0, 128), S("iwp" if t < 2 else "iw", 0, 128), AF.Identity, bias=C(GPX + t))
 
     def shift_lists(t):
-        ts(S("lst%d" % t, 0, 4), S("iw", 0, 4), C(GAP + t), 64.0, OP.subtract, OP.add)
-        ts(S("lb%d" % t, 4, 128), S("iw", 4, 128), C(GAP + t), None, OP.subtract)
+        if t < 2:
+            ts(S("lb%d" % t, 0, 128), S("iwl", 0, 128), C(GAP + t), float(CAP), OP.subtract, OP.min)
+        else:
+            ts(S("lb%d" % t, 4, 128), S("iw", 4, 128), C(GAP + t), None, OP.subtract)
+
+    def edge_list(t):
+        ts(S("lst%d" % t, 0, 4), S("iwe" if t < 2 else "iw", 0, 4), C(GAP + t), 64.0, OP.subtract, OP.add)
 
     def slots_a(t):
         n = 128 if t else 256
-        tt(S("st", 0, n), S("own%d" % (t > 0), 0, n), S("b3", 16, 16 + n), OP.max)
+        tt(S("st", 0, n), S("own%d" % (t > 0), 0, n), S("b1", 256, 256 + n), OP.max)
 
     def slots_b(t):
         n = 128 if t else 256
@@ -272,9 +336,9 @@ def rank_program(g, core, T, topo):
         fl, x = "fl%d" % t, "xc%d" % t
         out = []
         if rank > 0:
-            out.append((rank - 1, S(fl, 0, HALO), T[x][:, XW:XW + HALO], "ar%d" % t))
+            out.append((rank - 1, S(x, X0, X0 + HALO), T[x][:, 0:HALO], "ar%d" % t))
         if rank < nranks - 1:
-            out.append((rank + 1, S(fl, HALO, 2 * HALO), T[x][:, 0:HALO], "al%d" % t))
+            out.append((rank + 1, S(fl, 0, HALO), T[x][:, HALO:X0], "al%d" % t))
         reads = [a for o in out for a in o[1][1]]
         if len(out) == 1:
             dst = T.cores[out[0][0]]
@@ -296,209 +360,228 @@ def rank_program(g, core, T, topo):
         tr["remote"](reads, "sent", used, lambda: g.remote_dma_fused(trs, local_sem=T.sem.sent))
 
     for t in range(3):
-        for peer, key, lo in ((rank - 1, "al%d" % t, 0), (rank + 1, "ar%d" % t, XW)):
+        for peer, key, lo in ((rank - 1, "al%d" % t, HALO), (rank + 1, "ar%d" % t, 0)):
             if 0 <= peer < nranks:
                 en = len(topo.engines(T.cores[peer], core))
                 tr["landing"](key, en if peer in (0, nranks - 1) else en // 2, [("xc%d" % t, lo, lo + HALO)])
-
-    def scores(t, half):
-        ob = S("b0", 0, 64) if half == 0 else S("b2", 0, 64)
-        c0, s0 = 64 * half, zoff[t - 1] + 1024 * half
-        mms([(ob, S("idn", 0, 128), S("pen%d" % t, c0, c0 + 64), True, False)]
-            + [(ob, win("sv%d" % t, k), S("big", s0 + k, s0 + 1024, 16), False, k == 15) for k in range(16)])
 
     def back(eng, level, lo, hi):
         src, top = ((0, V1), (Z1, V2), (Z2, Z3))[level]
         i = W("big", src, top + min(hi, CAP), "slot%d" % level, lo // 16, hi // 16)
         o = S("yb", lo, hi) if level == 0 else S("big", (0, V1, V2)[level] + lo, (0, V1, V2)[level] + hi)
-        if eng == "a":
-            act(o, i, AF.Copy) if level != 1 else act(o, i, AF.Identity, bias=-OFS)
-        elif level != 1:
-            vcopy(o, i)
-        else:
-            ts(o, i, -OFS, None, OP.add)
+        gather(eng, o, i, -OFS if level == 1 else None)
 
     def store(lo, hi):
         emit("s", lambda: g.sync.dma_start(T.y[:, lo:hi], T.yb[:, lo:hi]), [("yb", lo, hi)], [], dma="dy%d" % (lo // 256))
 
+    def firsts(p, lo=0, step=1):
+        return S("b0", 256 + lo, 512, step) if p else S("b2", lo, 256, step)
+
+    def preset_firsts(p):
+        mms([(firsts(p), idn, S("cp", 0, 256), True, False), (firsts(p, 1, 2), idn, jrow, False, False)])
+
+    def preset_markers(p):
+        mms([(S("b1", 128 * p, 128 * p + 128), S("s15", 0, 128), S("jrow", 128 * p, 128 * p + 128), True, False)])
+
     for t in range(3):
-        rm, dw, xc, lst, fl, sv = ["%s%d" % (n, t) for n in ("rm", "dw", "xc", "lst", "fl", "sv")]
+        rm, dw, xc, lst, fl, sv, ls, lse = ["%s%d" % (n, t) for n in ("rm", "dw", "xc", "lst", "fl", "sv", "ls", "lse")]
         space = (0, 4096) if t == 0 else (zoff[t - 1], zoff[t - 1] + CAP)
         z = zoff[t]
         P0 = (16, 304) if t == 0 else (16,)
         last = len(P0) - 1
+        lcsel, kept = S("b2", 256, 384), S("b3", 300, 301)
 
-        def mark(p):
-            m0, r0, c0, w0, o = P0[p], P0[p] + 128, 128 * p, 8 * p, 32 * p
-            mms([(S("b1", c0, c0 + 128), S("lt", 0, 128), S(rm, m0, r0), True, False),
-                 (S("b1", c0, c0 + 128), S("s15", 0, 128), S("mrow", c0, c0 + 128), False, True)])
+        def mask(p):
+            ts(S(rm, P0[p], P0[p] + 128), S("b3" if p else "b0", 0, 128), C(TH + t), None, OP.is_ge)
+
+        def count(p):
+            m0, r0, c0 = P0[p], P0[p] + 128, 128 * p
+            mms([(firsts(p, 1, 2), S("nbd", 0, 128), S(rm, m0, r0), False, False)])
+            mms([(S("b1", c0, c0 + 128), S("lt", 0, 128), S(rm, m0, r0), False, True)])
             scan(S(rm, r0, r0 + 129), S(rm, m0 - 1, r0), S(rm, m0 - 1, r0), S(rm, P0[0] + 256, P0[0] + 257) if p else 0.0, OP.add, OP.max)
-            act(S("dsb", c0, c0 + 128), S("b1", c0, c0 + 128), AF.Copy)
+            mms([(firsts(p, 0, 2), bd, S(rm, r0, r0 + 128), False, True)])
             if p == last:
-                mms([(S("b3", 0, 1), S("bd", 0, 128), S(rm, r0 + 128, r0 + 129), True, True)])
-            b2, b2m = S("b2", o, o + 16), S("b2", o, o + 8)
-            rhs = [(win("e", k), S(rm, m0 + k, m0 + 256, 16)) for k in range(16)]
-            mms([(b2, rhs[0][0], rhs[0][1], True, False),
-                 (b2m, S("idn", 0, 128), S("chi", w0, w0 + 8), False, False), (b2m, S("idn", 0, 128), S("clo", w0, w0 + 8), False, False)]
-                + [(b2, rhs[k][0], rhs[k][1], False, k == 15) for k in range(1, 16)])
+                mms([(kept, bd, S(rm, r0 + 128, r0 + 129), True, True)])
 
-        def offsets(p, fill1=None, fill2=None):
-            w0, o = 8 * p, 32 * p
-            ts(S("of1", w0, w0 + 8), S("b2", o, o + 8), -8192.0, None, OP.mult)
-            if fill1:
-                fill1()
-            tt(S("of2", w0, w0 + 8), S("of1", w0, w0 + 8), S("b2", o + 8, o + 16), OP.max)
-            if fill2:
-                fill2()
-            vcopy(S("off%d" % t, w0, w0 + 8), S("of2", w0, w0 + 8))
+        def markers(p):
+            act(S("dsb", 128 * p, 128 * p + 128), S("b1", 128 * p, 128 * p + 128), AF.Relu, bias=C(RB))
+
+        def take(p):
+            scan(S("pk", 0, 256), S("rs", 0, 256), firsts(p), 0.0, OP.add, OP.max)
+
+        def offsets(p):
+            ts(S("off%d" % t, 8 * p, 8 * p + 8), S("pk", 31, 256, 32), -BIG, None, OP.add)
 
         def scatter(p):
-            vscatter(W(dw, 0, DWW, "off%d" % t, 8 * p, 8 * p + 8), S("dsb", 128 * p, 128 * p + 128))
+            vscatter(W(dw, M0, M0 + CAP + 128, "off%d" % t, 8 * p, 8 * p + 8), S("dsb", 128 * p, 128 * p + 128))
 
-        def pick(eng, out, lname, l0, l1):
-            i = W("big", *space, lname, l0, l1)
-            if eng == "a":
-                act(out, i, AF.Copy) if t == 0 else act(out, i, AF.Identity, bias=-OFS)
-            else:
-                vcopy(out, i) if t == 0 else ts(out, i, -OFS, None, OP.add)
+        def wrap(bank, lo, hi):
+            o, i = S(bank, 0, (hi - lo) // 16), int(t > 0)
+            mms([(o, win("nxt%de" % i, 0), S("u", lo - 1, hi - 1, 16), True, False)]
+                + [(o, win("two%de" % i if k < 15 else "own%de" % i, k), S("u", lo + k, hi, 16), False, k == 15) for k in range(16)])
+
+        def listed(bank, lo, hi):
+            ts(S(ls, lo // 16 - 1, hi // 16 - 1), S(bank, 0, (hi - lo) // 16), 15.0 * (128 if t else 1), None, OP.add)
+
+        def pick(eng, lo, hi):
+            gather(eng, S(xc, X0 + lo, X0 + hi), W("big", *space, ls, L0 + lo // 16, L0 + hi // 16), -OFS if t else None)
 
         def left(eng, lo, hi):
-            o, i = S("gb", lo, hi), W(xc, HALO, HALO + hi, "lb%d" % t, lo // 16, hi // 16)
-            act(o, i, AF.Copy) if eng == "a" else vcopy(o, i)
+            gather(eng, S("gb", lo, hi), W(xc, X0, XZ + 16 if t < 2 else X0 + hi, "lb%d" % t, lo // 16, hi // 16))
 
         def right(eng, lo, hi):
-            o, i = S("gc", lo, hi), W(xc, HALO, XW + HALO, "lc%d" % t, lo // 16, hi // 16)
-            act(o, i, AF.Copy) if eng == "a" else vcopy(o, i)
+            gather(eng, S("gc", lo, hi), W(xc, 0, XZ if t < 2 else min(XZ, X0 + hi + HALO), "lc%d" % t, lo // 16, hi // 16))
 
-        def bank(c):
-            return S(("b4", "b5", "b6", "b7", "b1")[c], 0, PARTS[c][1] - PARTS[c][0])
+        def edge(eng):
+            gather(eng, S("ge" if t < 2 else "gb", 0, HALO), W(xc, HALO, X0 + HALO, lst, 0, 4))
+
+        def rows(c):
+            return range(PARTS[c][0] // 128, PARTS[c][1] // 128)
+
+        def bank(c, k=None, lo=0, hi=128):
+            if c == 4:
+                return S(MIXB[c], lo, hi)
+            return (T[MIXB[c]][:, 0:len(rows(c)), lo:hi] if k is None else T[MIXB[c]][:, k - rows(c)[0], lo:hi]), [(MIXB[c], 0, 512)]
 
         def offset(c):
             mms([(bank(c), S("idb", 0, 128), S("ones", 0, PARTS[c][1] - PARTS[c][0]), True, False)])
 
         def mix(c, j):
             lo, hi = PARTS[c]
-            mms([(bank(c), tap(t, j), S(*((xc, HALO + lo, HALO + hi), ("gb", lo, hi), ("gc", lo, hi))[j]), False, j == 2)])
+            if j == 0 and t < 2:
+                mms([(bank(c, k), tap(t, 0), S(xc, X0 + k, XZ, 16), False, False) for k in rows(c)])
+            else:
+                mms([(bank(c), tap(t, j), S(*((xc, X0 + lo, X0 + hi), ("gb", lo, hi), ("gc", lo, hi))[j]), False, j == 2)])
+
+        def centre(c, half):
+            lo = X0 + 1024 * half
+            mms([(bank(c, k, 64 * half, 64 * half + 64), tap(t, 0), S(xc, lo + k, lo + 1024, 16), False, False) for k in rows(c)])
+
+        def mix_edge(c):
+            mms([(bank(c, None, 0, 4), tap(t, 1), S("ge", 4 * rows(c)[0], 4 * rows(c)[-1] + 4), False, False)])
 
         def near(c):
             lo, hi = PARTS[c]
             ts(S("big", z + lo, z + hi), bank(c), OFS - 15.0, OFS + 15.0, OP.max, OP.min)
 
-        if t == 0:
-            for c in range(4):
-                wrap(S("b0" if c < 2 else "b3", 64 * (c % 2), 64 * (c % 2) + 64), sv, "big", 1024 * c, 1024 * c + 1024)
-                if c == 1:
-                    ts(S(rm, 16, 144), S("b0", 0, 128), C(TH), None, OP.is_ge)
-                if c == 2:
-                    tap_matrices(0, 2)
-                    mark(0)
-            shift_lists(0)
-            for name, c in (("idk", 8192.0), ("idb", OFS)):
-                ts(S(name, 0, 128), S("idn", 0, 128), c, None, OP.mult)
-            offsets(0)
-            ts(S(rm, 304, 432), S("b3", 0, 128), C(TH), None, OP.is_ge)
-        else:
-            scores(t, 1)
-            shift_lists(t)
-            slots_a(t - 1)
-            ts(S(rm, 16, 80), S("b0", 0, 64), C(TH + t), None, OP.is_ge)
-            ts(S(rm, 80, 144), S("b2", 0, 64), C(TH + t), None, OP.is_ge)
-        mark(last)
-        if t == 0:
-            scatter(0)
-        else:
-            slots_b(t - 1)
-        act(C(KR), S("b3", 0, 1), AF.Copy)
-        act(C(KC), S("b3", 0, 1), AF.Copy, bias=float(XW - HALO), scale=-1.0)
-        lcsel = S("b0", 256, 384)
-        offsets(last, lambda: ts(lcsel, S("iwd%d" % t, 0, 128), C(KR), C(KC), OP.is_ge, OP.mult),
-                lambda: ts(S(lst, 4, 8), S("qk", 0, 4), C(KR), None, OP.add))
-        scatter(last)
-        for p in range(last + 1):
-            cum, m0 = S("b3", 16 + 128 * p, 144 + 128 * p), P0[p]
-            mms([(cum, S("bd", 0, 128), S(rm, m0 + 128, m0 + 256), True, False), (cum, S("ltf", 0, 128), S(rm, m0, m0 + 128), False, False),
-                 (cum, S("idk", 0, 128), S(rm, m0, m0 + 128), False, True)])
-        if t == 0:
-            tap_matrices(2, 8)
-            mms([(S("b3", 300, 303), S("bd", 0, 128), S("vb", 0, 3), True, True)])
-        u0 = 0.0
-        for lo, hi in ((0, 512), (512, 1024), (1024, 2048)):
-            scan(S("u", lo, hi), S("dc", lo, hi), S(dw, lo, hi), u0, OP.add, OP.max)
-            if lo < 1024:
-                act(S("cb", lo, hi), S("u", lo, hi), AF.Relu, bias=C(BI), scale=C(SC))
-            if lo == 0:
-                tt(S("lcf", 0, 128), S("iwd%d" % t, 0, 128), lcsel, OP.add)
-            if lo == 512:
-                ts(S("cf", 0, 64), S("u", 0, 64), C(BMIN), None, OP.min)
-            if lo == 1024:
-                ts(S("lc%d" % t, 0, 128), S("lcf", 0, 128), float(CAP + HALO - 1), None, OP.min)
-            u0 = S("u", hi - 1, hi)
-        ts(S("cf", 64, 128), W("u", 0, CAP, lst, 4, 8), C(BMIN), None, OP.min)
-        for c in range(3):
-            offset(c)
-        wrap(S("b1", 0, 32), "el1", "cb", 0, 512)
-        wrap(S("b2", 0, 8), "el2", "cf", 0, 128)
-        vcopy(S("la%d" % t, 0, 32), S("b1", 0, 32))
-        pick("a", S(xc, 64, 576), "la%d" % t, 0, 32)
-        ts(S("cb", 1024, 2048), S("u", 1024, 2048), C(BMIN), None, OP.min)
-        ts(S("fll%d" % t, 0, 8), S("b2", 0, 8), 15.0, None, OP.add)
-        pick("v", S(fl, 0, 128), "fll%d" % t, 0, 8)
-        send(t)
-        wrap(S("b1", 0, 32), "el1", "cb", 512, 1024)
-        wrap(S("b0", 0, 64), "el2", "cb", 1024, 2048)
-        vcopy(S("lm%d" % t, 0, 32), S("b1", 0, 32))
-        pick("a", S(xc, 576, 1088), "lm%d" % t, 0, 32)
-        ts(S("ll%d" % t, 0, 64), S("b0", 0, 64), 15.0, None, OP.add)
-        pick("v", S(xc, 1088, 64 + CUT), "ll%d" % t, 0, CUT // 16 - 64)
-        pick("a", S(xc, 64 + CUT, 2112), "ll%d" % t, CUT // 16 - 64, 64)
-        offset(3)
-        offset(4)
-        left("a", 64, 512)
-        left("v", 1024, 1536)
-        left("a", 512, 1024)
-        left("v", 1536, 2048)
-        for c in range(5):
-            mix(c, 0)
-        vcopy(S("gb", 0, 64), W(xc, 0, HALO + 64, lst, 0, 4))
-        right("a", 0, 512)
-        for c in (2, 1, 3, 4, 0):
-            mix(c, 1)
-        right("v", 1536, 1920)
-        mix(0, 2)
-        right("a", 512, 1024)
-        mix(3, 2)
-        right("a", 1024, 1536)
-        mix(1, 2)
-        if t < 2:
-            ts(S("pen%d" % (t + 1), 0, 128), S("iw", 0, 128), C(KR), -32768.0, OP.is_ge, OP.mult)
-        else:
-            slots_a(2)
-        right("a", 1920, 2048)
-        if t == 0:
-            later_constants()
-        mix(2, 2)
-        mix(4, 2)
-        if t == 2:
-            slots_b(2)
-        near(0)
-        if t == 2:
-            back("a", 2, 0, 512)
-        near(3)
-        near(1)
-        if t == 2:
-            back("a", 1, 0, 512)
-        if t < 2:
-            scores(t + 1, 0)
-        near(2)
-        near(4)
-        if t == 0:
-            gfill("dw2", 0, CAP, 0)
+        def score(c, stop=False):
+            mms([(S("b0", 0, 128), win("sv%d" % (t + 1), k), S("big", z + 128 * k, z + 128 * k + 128), False, stop and k == rows(c)[-1])
+                 for k in rows(c)])
 
-    for level, c in ((2, 1), (0, 0), (1, 1), (2, 2), (0, 1), (1, 2), (2, 3), (0, 2), (1, 3), (0, 3), (0, 4), (0, 5), (0, 6), (0, 7)):
-        for lo, hi in ((512 * c, 512 * c + 512),) if (level, c) != (0, 7) else ((3584, 3840), (3840, 4096)):
-            mid = (lo + hi) // 2
-            back("a", level, lo, mid)
-            back("v", level, mid, hi)
-            if level == 0:
-                store(lo, hi)
+        def scores0(c):
+            o = S("b0" if c < 2 else "b3", 64 * (c % 2), 64 * (c % 2) + 64)
+            mms([(o, win(sv, k), S("big", 1024 * c + k, 1024 * c + 1024, 16), k == 0, k == 15) for k in range(16)])
+
+        def counts():
+            for p in range(last + 1):
+                cum, m0 = S("b1", 256 + 128 * p, 384 + 128 * p), P0[p]
+                mms([(cum, bd, S(rm, m0 + 128, m0 + 256), True, False), (cum, S("ltf", 0, 128), S(rm, m0, m0 + 128), False, False),
+                     (cum, S("idk", 0, 128), S(rm, m0, m0 + 128), False, True)])
+
+        if t == 0:
+            scores0(0)
+            scores0(1)
+            preset_firsts(0)
+            preset_markers(0)
+            scores0(2)
+            mask(0)
+            small_columns(0)
+            count(0)
+            place_rows()
+            markers(0)
+            steps_row()
+            list_matrices("v", 0)
+            take(0)
+            small_columns(1)
+            offsets(0)
+            scores0(3)
+            preset_firsts(1)
+            preset_markers(1)
+            if PAR.get("early"):
+                scatter(0)
+            mask(1)
+            scaled("v", S("idm", 0, 128), idn, -BIG)
+            count(1)
+            markers(1)
+            if not PAR.get("early"):
+                scatter(0)
+            take(1)
+            scaled("v", S("sv1", 0, 144), e, C(VF + 1))
+        else:
+            mask(0)
+            slots_a(t - 1)
+            count(0)
+            markers(0)
+            shift_lists(t)
+            edge_list(t)
+            take(0)
+            slots_b(t - 1)
+        offsets(last)
+        ts(S(lse, 0, 5), S("qk", 0, 5), kept, -float(HALO), OP.add, OP.add)
+        scatter(last)
+        act(C(KS), kept, AF.Copy, bias=float(X0))
+        if t < 2:
+            act(C(KP), kept, AF.Copy, bias=1.0, scale=-1.0)
+        if t == 0:
+            scaled("v", S("idk", 0, 128), idn, 8192.0)
+            edge_places()
+            tap_matrices()
+        if t < 2:
+            act(S("pen", 0, 128), S("iw", 0, 128), AF.Relu, bias=C(KP))
+        cuts = [16] + [M0 + c for c in PAR["cuts"]] + [M0 + CAP]
+
+        def carry(i):
+            lo, hi = max(cuts[i], M0), cuts[i + 1]
+            scan(S("u", lo, hi), S("dc", 0, hi - lo), S(dw, lo, hi), S("u", lo - 1, lo) if i else 0.0, OP.add, OP.max)
+
+        def leave():
+            send(t)
+            if t < 2:
+                gfill("dw%d" % (t + 1), M0 - 16, M0 + CAP, 0)
+            if t == 0:
+                shift_lists(0)
+                edge_list(0)
+
+        def ahead():
+            if t == 0:
+                later_constants()
+            right_base(t + 1)
+
+        def penalty():
+            if t == 0:
+                mms([(S("b2", 400, 403), bd, S("vb", 0, 3), True, True)])
+            mms([(S("b0", 0, 128), S("idm", 0, 128), S("pen", 0, 128), True, False)])
+
+        def preset():
+            preset_firsts(0)
+            preset_markers(0)
+
+        ranged = {"p": pick, "l": left, "r": right, "y": lambda eng, lo, hi: store(lo, hi)}
+        for level in range(3):
+            ranged[str(level)] = lambda eng, lo, hi, level=level: back(eng, level, lo, hi)
+        chunked = {"o": offset, "A": lambda c: mix(c, 0), "F": lambda c: centre(c, 0), "G": lambda c: centre(c, 1), "B": lambda c: mix(c, 1),
+                   "C": lambda c: mix(c, 2), "E": mix_edge, "n": near, "s": score, "S": lambda c: score(c, True),
+                   "u": carry, "W": lambda i: wrap("b%d" % (1 - i % 2), cuts[i], cuts[i + 1]),
+                   "L": lambda i: listed("b%d" % (1 - i % 2), cuts[i], cuts[i + 1])}
+        named = {"tail": lambda: vcopy(S(dw, 0, TAIL), W(dw, M0 - 16, M0 + CAP, lse, 0, 5)),
+                 "utail": lambda: scan(S("u", 0, TAIL), S("dc", 0, TAIL), S(dw, 0, TAIL), 0.0, OP.add, OP.max),
+                 "lastv": lambda: gather("v", S(fl, 0, HALO), W("big", *space, ls, 0, 4), -OFS if t else None),
+                 "lasta": lambda: gather("a", S(fl, 0, HALO), W("big", *space, ls, 0, 4), -OFS if t else None),
+                 "send": leave,
+                 "lc1": lambda: ts(lcsel, S("iwd%d" % t, 0, 128), C(KS), C(KS), OP.is_ge, OP.mult),
+                 "lc2": lambda: tt(S("lcf", 0, 128), S("iwd%d" % t, 0, 128), lcsel, OP.subtract),
+                 "lc3": lambda: vcopy(S("lc%d" % t, 0, 128), S("lcf", 0, 128)),
+                 "counts": counts, "slots": lambda: slots_a(t), "slots2": lambda: slots_b(t),
+                 "edgev": lambda: edge("v"), "edgea": lambda: edge("a"), "base": ahead, "preset": preset, "pen": penalty}
+        for step in PAR["mid" if t < 2 else "end"].split():
+            if step in named:
+                named[step]()
+            elif "-" in step:
+                lo, hi = [int(c) for c in step[2:].split("-")]
+                mid = (lo + hi) // 32 * 16
+                for eng, a, b in (((step[1], lo, hi),) if step[1] != "x" else (("a", lo, mid), ("v", mid, hi))):
+                    ranged[step[0]](eng, a, b)
+            else:
+                for c in step[1:]:
+                    chunked[step[0]](int(c))
     tr["finish"]()

from concourse.bass import DstId, RemoteDMATransfer
from concourse.mybir import AluOpType, ActivationFunctionType

OP = AluOpType
AF = ActivationFunctionType
CAP, HALO, OFS, BIG = 2048, 64, 192.0, 32768.0
X0 = 2 * HALO
XZ = X0 + CAP
V1, Z1, V2, Z2, Z3, BIGW = 4096, 6144, 8192, 10240, 12288, 14336
TAIL, M0 = 80, 112
L0 = (M0 - 16) // 16
RMW = 576
PARTS = [(0, 512), (512, 1024), (1024, 1536), (1536, 1920), (1920, 2048)]
MIXB = ("b4", "b5", "b6", "b7", "b3")
_LIST = "o0123 tail u0 utail u1 W01 L0 lc1 pa0-64 lastv send pa64-640 lc2 lc3 L1 pa640-1280 pv1280-2048 counts "
PAR = {"cuts": [640], "fill": 1024,
       "mid": _LIST + """pen A0123 o4 A4 la0-512 lv1024-1536 la512-1024 lv1536-2048 B0213 edgev E0 ra0-256 rv256-512 C0
           ra512-1024 rv1024-1408 E1 C1 n0 B4 E234 ra1408-1536 C2 ra1536-1920 n1 s0 C3 ra1920-2048 n2 base s1 C4 n3 preset s2 n4 s3 S4""",
       "end": _LIST + """o4 la64-512 slots lv1024-1536 la512-1024 slots2 lv1536-2048 A01234 edgev B21340
           rx0-512 C0 ra512-1024 rv1024-1536 C12 n0 ra1536-1920 C3 n1 ra1920-2048 C4 2a0-512 n2 n3 1a0-512 n4
           2v512-1024 0a0-512 y.0-512 2v1024-1536 1a512-1024 2v1536-2048 0a512-1024 y.512-1024 1v1024-1536 1a1536-2048
           0v1024-1536 y.1024-1536 0a1536-2048 y.1536-2048 0x2048-2560 y.2048-2560 0x2560-3072 y.2560-3072 0x3072-3584 y.3072-3584
           0x3584-3840 y.3584-3840 0x3840-4096 y.3840-4096"""}

_W = {"bfloat16": {"big": BIGW, "gb": CAP, "gc": CAP, "ge": HALO, "u": M0 + CAP, "dc": 1408, "dsb": 256, "jrow": 256, "jg": 128, "jk": 128,
                   "e": 144, "bd": 128, "nbd": 128, "idn": 128, "idk": 128, "idb": 128, "idm": 128, "ltf": 128, "lt": 128, "s15": 128,
                   "own0e": 144, "own1e": 144, "nxt0e": 144, "nxt1e": 144, "two0e": 144, "two1e": 144,
                   "cp": 256, "rs": 256, "ones": 512, "vb": 3, "pen": 128},
      "float32": {"yb": 4096, "iw": 128, "iwp": 128, "iwl": 128, "iwe": 4, "own0": 256, "own1": 128,
                  "gm": 8, "cc": 64, "pk": 256, "st": 256, "qk": 5, "lcf": 128},
      "int32": {"ip": 1, "gi": 1, "ki": 1, "ei": 1, "thi": 3, "gpi": 3}, "uint16": {}}
for _t in range(3):
    for _n, _k, _d in (("xc", XZ + 16, "bfloat16"), ("fl", HALO, "bfloat16"), ("dw", M0 + CAP + 128, "bfloat16"), ("rm", RMW, "bfloat16"),
                       ("sv", 144, "bfloat16"), ("iwd", 128, "float32"),
                       ("lb", 128, "uint16"), ("lc", 128, "uint16"), ("lst", 4, "uint16"), ("lse", 6, "uint16"),
                       ("off", 16, "uint16"), ("ls", L0 + 128, "uint16"), ("slot", 128 if _t else 256, "uint16")):
        _W[_d]["%s%d" % (_n, _t)] = _k
SCRATCH = {n: ("sbuf", [128, k], d) for d, a in _W.items() for n, k in a.items()}
SCRATCH["wb"] = ("sbuf", [128, 9, 16], "bfloat16")
SCRATCH["wbd"] = ("sbuf", [128, 9, 128], "bfloat16")
BANKS = ["b%d" % i for i in range(8)]
for _b in BANKS:
    SCRATCH[_b] = ("psum", [128, 4, 128] if _b in MIXB[:4] else [128, 512], "float32")
SEMAPHORES = (["cv", "ca", "cp", "cg", "dv", "dt", "dg", "dwt", "sent"] + ["dx%d" % i for i in range(4)]
              + ["dy%d" % i for i in range(16)] + ["al%d" % i for i in range(3)] + ["ar%d" % i for i in range(3)])
PF, GF, KF, G15, K15, K00, K16, ND, RB, W0, R4, E0, OW0, OW1, NX0, NX1, OWN0, OWN1, KS, KP = range(20)
TH, GAP, GPX, VF = 24, 27, 30, 33


def tracker(g, T):
    queues = {"v": g.vector, "a": g.scalar, "p": g.tensor, "g": g, "s": g.sync}
    count, clock, order, recs, waited = {}, {}, {}, {}, {}
    known = {e: {} for e in queues}
    serial = [0]

    def wait(eng, key, n):
        if known[eng].get(key, 0) >= n:
            return
        queues[eng].wait_ge(T.sem[key], n)
        waited[key] = max(waited.get(key, 0), n)
        for k2, n2 in clock.get((key, n), {}).items():
            known[eng][k2] = max(known[eng].get(k2, 0), n2)
        known[eng][key] = n

    def settle(eng, reads, writes):
        need = {}
        for kind, accs in (("r", reads), ("w", writes)):
            for b, lo, hi in accs:
                ps = b in BANKS
                for rk, rlo, rhi, who, key, n in recs.get(b, ()):
                    over = rlo < hi and lo < rhi
                    if who == eng:
                        if eng == "p" or not over or rk == kind == "r":
                            continue
                    elif not ps and (not over or rk == kind == "r"):
                        continue
                    need[key] = max(need.get(key, 0), n)
        for key in sorted(need, key=lambda k: -order[(k, need[k])]):
            wait(eng, key, need[key])

    def note(who, key, n, reads, writes):
        serial[0] += 1
        order[(key, n)] = serial[0]
        for kind, accs in (("r", reads), ("w", writes)):
            for b, lo, hi in accs:
                recs.setdefault(b, []).append((kind, lo, hi, who, key, n))

    def emit(eng, fn, reads, writes, dma=None):
        settle(eng, reads, writes)
        key, step = (dma, 16) if dma else ("c" + eng, 1)
        n = count.get(key, 0) + step
        fn().then_inc(T.sem[key], step)
        count[key] = n
        clock[(key, n)] = dict(known[eng])
        note("dma " + dma if dma else eng, key, n, reads, writes)

    def remote(reads, key, n, fn):
        settle("g", reads, [])
        fn()
        count[key] = count.get(key, 0) + n
        note("net " + key, key, count[key], reads, [])

    def landing(key, n, writes):
        count[key] = n
        note("net " + key, key, n, [], writes)

    def finish():
        for key in sorted(count):
            if waited.get(key, 0) < count[key]:
                wait("s", key, count[key])

    return {"emit": emit, "remote": remote, "landing": landing, "finish": finish}


def rank_program(g, core, T, topo):
    rank = T.rank_of(core)
    if rank is None:
        return
    tr = tracker(g, T)
    emit = tr["emit"]
    nranks = len(T.cores)

    def S(name, lo, hi, step=1):
        if step == 1:
            return T[name][:, lo:hi], [(name, lo, hi)]
        return T[name][:, lo:hi:step], [(name, lo, hi)]

    def W(name, lo, hi, lname, l0, l1):
        return T[name][:, lo:hi].indirect(T[lname][:, l0:l1]), [(name, lo, hi), (lname, l0, l1)]

    def C(col):
        return S("cc", col, col + 1)

    def split(x):
        return (x[0], x[1]) if isinstance(x, tuple) else (x, [])

    def ts(out, in0, s1, s2, op0, op1=None):
        (a1, r1), (a2, r2) = split(s1), split(s2)
        if op1 is None:
            emit("v", lambda: g.vector.tensor_scalar(out[0], in0[0], a1, None, op0), in0[1] + r1, out[1])
        else:
            emit("v", lambda: g.vector.tensor_scalar(out[0], in0[0], a1, a2, op0, op1), in0[1] + r1 + r2, out[1])

    def tt(out, in0, in1, op):
        emit("v", lambda: g.vector.tensor_tensor(out[0], in0[0], in1[0], op), in0[1] + in1[1], out[1])

    def vcopy(out, in_):
        emit("v", lambda: g.vector.tensor_copy(out[0], in_[0]), in_[1], out[1])

    def vscatter(win, in_):
        emit("v", lambda: g.vector.tensor_copy(win[0], in_[0]), in_[1] + win[1][1:], win[1][:1])

    def vfill(out, c):
        emit("v", lambda: g.vector.memset(out[0], c), [], out[1])

    def scan(out, d0, d1, init, op0, op1):
        ai, ri = split(init)
        emit("v", lambda: g.vector.tensor_tensor_scan(out[0], d0[0], d1[0], ai, op0, op1), d0[1] + d1[1] + ri, out[1])

    def act(out, in_, func, bias=0.0, scale=1.0):
        (ab, rb), (asc, rs) = split(bias), split(scale)
        emit("a", lambda: g.scalar.activation(out[0], in_[0], func, bias=ab, scale=asc), in_[1] + rb + rs, out[1])

    def mms(items):
        def go():
            last = None
            for o, l, r, a, b in items:
                last = g.tensor.matmul(o[0], l[0], r[0], a, b)
            return last
        emit("p", go, sorted({a for i in items for a in i[1][1] + i[2][1]}), sorted({a for i in items for a in i[0][1]}))

    def iota(name, lo, hi, pattern, base, cm):
        if name == "ip":
            emit("g", lambda: g.iota(T[name][:, lo:hi], pattern, base, cm), [], [(name, lo, hi)])
        else:
            emit("g", lambda: g.iota(T[name][:, lo:hi], pattern, base, cm, allow_small_or_imprecise_dtypes=True), [], [(name, lo, hi)])

    def gfill(name, lo, hi, value):
        iota(name, lo, hi, [[0, hi - lo]], value, 0)

    def load(eng, sem, out, src):
        q = g.sync if eng == "s" else g.scalar
        emit(eng, lambda: q.dma_start(out[0], src), [], out[1], dma=sem)

    def gather(eng, out, i, add=None):
        if eng == "a":
            act(out, i, AF.Copy) if add is None else act(out, i, AF.Identity, bias=add)
        else:
            vcopy(out, i) if add is None else ts(out, i, add, None, OP.add)

    def scaled(eng, out, in_, by):
        act(out, in_, AF.Copy, scale=by) if eng == "a" else ts(out, in_, by, None, OP.mult)

    def win(name, k):
        return S(name, 15 - k, 143 - k)

    def tap(t, j):
        i = 3 * t + j
        return T.wbd[:, i, :], [("wbd", i, i + 1)]

    load("a", "dv", S("vb", 0, 3), T.v[:])
    for c in range(4):
        load("s", "dx%d" % c, S("big", 1024 * c, 1024 * c + 1024), T.x[:, 1024 * c:1024 * c + 1024])
    load("a", "dt", S("thi", 0, 3), T.th[:])
    load("a", "dg", S("gpi", 0, 3), T.gap[:])
    load("a", "dwt", (T.wb[:, :, :], [("wb", 0, 9)]), T.w[:])

    jrow, bd, e, idn = S("jrow", 0, 128), S("bd", 0, 128), S("e", 0, 144), S("idn", 0, 128)
    dcw = max(b - a for a, b in zip([0] + PAR["cuts"], PAR["cuts"] + [CAP]))
    base = [4096 - 1 - 8192, 2048 - 1 - 8192]
    weights = ((1.0, 16.0), (128.0, 1.0))
    iota("ip", 0, 1, [[0, 1]], 0, 1)
    iota("jrow", 0, 144, [[1, 144]], 0, 0)
    iota("jk", 0, 128, [[0, 8], [1, 16]], 0, 0)
    iota("jg", 0, 128, [[1, 8], [0, 16]], 0, 0)
    iota("jrow", 144, 256, [[1, 112]], 144, 0)
    iota("iwp", 0, 128, [[1, 16], [256, 8]], 0, 0)
    gfill("dw0", M0 + PAR["fill"], M0 + CAP, 0)
    gfill("u", TAIL, M0, 0)
    gfill("ones", 0, 512, 1)
    for t in range(3):
        if rank == 0:
            gfill("xc%d" % t, HALO, X0, 0)
        if rank == nranks - 1:
            gfill("xc%d" % t, 0, HALO, 0)
        if t:
            gfill("rm%d" % t, 15, 16, 0)
        if t < 2:
            gfill("xc%d" % t, XZ, XZ + 16, 0)
    vfill(S("rs", 0, 256), 0.0)
    ts(S("gi", 0, 1), S("ip", 0, 1), 4, None, OP.logical_shift_right)
    ts(S("ki", 0, 1), S("ip", 0, 1), 15, None, OP.bitwise_and)
    vfill(S("rs", 0, 256, 32), -2 * BIG)
    vcopy(C(GF), S("gi", 0, 1))
    vcopy(C(KF), S("ki", 0, 1))
    vcopy(C(PF), S("ip", 0, 1))
    ts(C(G15), C(GF), 16.0, 15.0, OP.mult, OP.add)
    ts(C(K15), C(KF), 15.0, None, OP.is_equal)
    ts(C(K00), C(KF), 0.0, None, OP.is_equal)
    ts(e, S("jrow", 0, 144), C(G15), None, OP.is_equal)
    ts(C(RB), C(K15), C(K00), -1.0, OP.add, OP.add)
    ts(idn, jrow, C(PF), None, OP.is_equal)
    vfill(S("rm0", 15, 304, 288), 0.0)
    act(C(W0), C(KF), AF.Copy, bias=15.0, scale=-1.0)
    act(C(K16), C(KF), AF.Copy, scale=16.0)
    act(C(ND), C(K00), AF.Identity, bias=C(RB), scale=-256.0)
    for i, (wp, wb) in enumerate(weights):
        act(C(OW0 + i), C(K15), AF.Copy, bias=wp, scale=wb - wp)
        act(C(NX0 + i), C(RB), AF.Copy, scale=wp)
        act(C(OW0 + i), C(K00), AF.Identity, bias=C(OW0 + i), scale=-2 * wp)
    ts(S("ltf", 0, 128), S("jk", 0, 128), C(KF), None, OP.is_ge)
    ts(S("sv0", 0, 144), e, S("vb", 0, 1), None, OP.mult)
    for i in (0, 1):
        ts(S("cp", i, 256, 2), S("jk", 0, 128), C(KF), BIG + CAP * i, OP.is_equal, OP.mult)
    ts(bd, S("jg", 0, 128), C(GF), None, OP.is_equal)
    ts(S("s15", 0, 128), idn, C(K15), None, OP.mult)
    tt(S("ltf", 0, 128), S("ltf", 0, 128), bd, OP.mult)
    act(S("nbd", 0, 128), bd, AF.Copy, scale=-8192.0)
    vcopy(S("cc", TH, TH + 3), S("thi", 0, 3))
    tt(S("lt", 0, 128), S("ltf", 0, 128), S("e", 0, 128), OP.subtract)
    ts(S("qk", 0, 5), S("jrow", 0, 5), 16.0, C(KF), OP.mult, OP.add)
    ts(S("lt", 0, 128, 16), S("bd", 0, 128, 16), C(W0), None, OP.mult)
    act(S("dw0", M0 - 16, M0 + PAR["fill"]), S("big", 0, PAR["fill"] + 16), AF.Copy, scale=0.0)

    def steps_row():
        act(S("dc", 0, dcw), S("big", 0, dcw), AF.Identity, bias=C(ND), scale=0.0)

    def list_matrices(eng, i):
        own, nxt, two = ["%s%de" % (n, i) for n in ("own", "nxt", "two")]
        scaled(eng, S(two, 0, 144), e, C(OW0 + i))
        scaled(eng, S(nxt, 0, 144), e, C(NX0 + i))
        scaled(eng, S(own, 0, 144), e, C(OW0 + i))
        scaled(eng, S(two, 16, 144, 16), S("bd", 0, 128, 16), C(NX0 + i))

    def tap_matrices():
        for i in range(8):
            emit("a", lambda: g.scalar.activation(T.wbd[:, :, 16 * i:16 * i + 16], T.wb[:, :, :], AF.Copy, scale=T.gm[:, i:i + 1]),
                 [("wb", 0, 9), ("gm", i, i + 1)], [("wbd", 0, 9)] if i == 7 else [])

    def small_columns(part):
        if part == 0:
            vcopy(S("cc", GAP, GAP + 3), S("gpi", 0, 3))
            ts(S("ei", 0, 1), S("ki", 0, 1), 2, None, OP.logical_shift_right)
            ts(C(R4), C(KF), 4.0, 4096.0, OP.is_lt, OP.mult)
        else:
            vcopy(C(E0), S("ei", 0, 1))
            ts(S("gm", 0, 8), S("jrow", 0, 8), C(GF), 0.125, OP.is_equal, OP.mult)
            vcopy(S("cc", VF, VF + 3), S("vb", 0, 3))

    def place_rows():
        act(S("idb", 0, 128), idn, AF.Copy, scale=OFS)
        act(S("iwp", 0, 128), S("iwp", 0, 128), AF.Identity, bias=C(K16))
        act(S("cc", GPX, GPX + 3), S("cc", GAP, GAP + 3), AF.Copy, bias=float(X0))
        act(S("iwl", 0, 128), S("iwp", 0, 128), AF.Copy)
        right_base(0)
        act(S("iwl", 0, 128, 8), S("iwp", 0, 128, 8), AF.Identity, bias=C(R4))

    def edge_places():
        act(C(E0), C(E0), AF.Identity, bias=C(K16), scale=-63.0)
        act(S("iw", 0, 128), jrow, AF.Identity, bias=C(KF), scale=16.0)
        act(S("iwe", 0, 4), S("jrow", 0, 4), AF.Identity, bias=C(E0), scale=4.0)

    def later_constants():
        for i in (1, 2):
            act(C(TH + i), S("b2", 400 + i, 401 + i), AF.Identity, bias=C(TH + i), scale=OFS)
        act(C(OWN0), C(KF), AF.Copy, bias=float(-base[0]))
        act(C(OWN1), C(KF), AF.Copy, bias=float(-base[1]), scale=128.0)
        act(S("own0", 0, 256), S("jrow", 0, 256), AF.Identity, bias=C(OWN0), scale=16.0)
        list_matrices("a", 1)
        act(S("own1", 0, 128), jrow, AF.Identity, bias=C(OWN1))
        act(S("sv2", 0, 144), e, AF.Copy, scale=C(VF + 2))

    def right_base(t):
        act(S("iwd%d" % t, 0, 128), S("iwp" if t < 2 else "iw", 0, 128), AF.Identity, bias=C(GPX + t))

    def shift_lists(t):
        if t < 2:
            ts(S("lb%d" % t, 0, 128), S("iwl", 0, 128), C(GAP + t), float(CAP), OP.subtract, OP.min)
        else:
            ts(S("lb%d" % t, 4, 128), S("iw", 4, 128), C(GAP + t), None, OP.subtract)

    def edge_list(t):
        ts(S("lst%d" % t, 0, 4), S("iwe" if t < 2 else "iw", 0, 4), C(GAP + t), 64.0, OP.subtract, OP.add)

    def slots_a(t):
        n = 128 if t else 256
        tt(S("st", 0, n), S("own%d" % (t > 0), 0, n), S("b1", 256, 256 + n), OP.max)

    def slots_b(t):
        n = 128 if t else 256
        ts(S("slot%d" % t, 0, n), S("st", 0, n), float(base[t > 0]), None, OP.add)

    zoff = [Z1, Z2, Z3]

    def send(t):
        fl, x = "fl%d" % t, "xc%d" % t
        out = []
        if rank > 0:
            out.append((rank - 1, S(x, X0, X0 + HALO), T[x][:, 0:HALO], "ar%d" % t))
        if rank < nranks - 1:
            out.append((rank + 1, S(fl, 0, HALO), T[x][:, HALO:X0], "al%d" % t))
        reads = [a for o in out for a in o[1][1]]
        if len(out) == 1:
            dst = T.cores[out[0][0]]
            a = topo.addr(dst)
            tr["remote"](reads, "sent", len(topo.engines(core, dst)), lambda: g.remote_dma(
                out_ap=out[0][2], in_ap=out[0][1][0], remote_sem=T.sem[out[0][3]], local_sem=T.sem.sent,
                pid=a[1], routing_id=a[0], dma_engine_mask=topo.mask(core, dst)))
            return
        trs, used = [], 0
        for i, o in enumerate(out):
            dst = T.cores[o[0]]
            a = topo.addr(dst)
            en = topo.engines(core, dst)
            half = len(en) // 2
            mine = en[:half] if i == 0 else en[half:]
            used += len(mine)
            trs.append(RemoteDMATransfer(dst_ids=[DstId(rid=a[0], pnc=a[1])], dma_engine_mask=sum(1 << k for k in mine),
                                         remote_sem=T.sem[o[3]], src=o[1][0], dst=o[2]))
        tr["remote"](reads, "sent", used, lambda: g.remote_dma_fused(trs, local_sem=T.sem.sent))

    for t in range(3):
        for peer, key, lo in ((rank - 1, "al%d" % t, HALO), (rank + 1, "ar%d" % t, 0)):
            if 0 <= peer < nranks:
                en = len(topo.engines(T.cores[peer], core))
                tr["landing"](key, en if peer in (0, nranks - 1) else en // 2, [("xc%d" % t, lo, lo + HALO)])

    def back(eng, level, lo, hi):
        src, top = ((0, V1), (Z1, V2), (Z2, Z3))[level]
        i = W("big", src, top + min(hi, CAP), "slot%d" % level, lo // 16, hi // 16)
        o = S("yb", lo, hi) if level == 0 else S("big", (0, V1, V2)[level] + lo, (0, V1, V2)[level] + hi)
        gather(eng, o, i, -OFS if level == 1 else None)

    def store(lo, hi):
        emit("s", lambda: g.sync.dma_start(T.y[:, lo:hi], T.yb[:, lo:hi]), [("yb", lo, hi)], [], dma="dy%d" % (lo // 256))

    def firsts(p, lo=0, step=1):
        return S("b0", 256 + lo, 512, step) if p else S("b2", lo, 256, step)

    def preset_firsts(p):
        mms([(firsts(p), idn, S("cp", 0, 256), True, False), (firsts(p, 1, 2), idn, jrow, False, False)])

    def preset_markers(p):
        mms([(S("b1", 128 * p, 128 * p + 128), S("s15", 0, 128), S("jrow", 128 * p, 128 * p + 128), True, False)])

    for t in range(3):
        rm, dw, xc, lst, fl, sv, ls, lse = ["%s%d" % (n, t) for n in ("rm", "dw", "xc", "lst", "fl", "sv", "ls", "lse")]
        space = (0, 4096) if t == 0 else (zoff[t - 1], zoff[t - 1] + CAP)
        z = zoff[t]
        P0 = (16, 304) if t == 0 else (16,)
        last = len(P0) - 1
        lcsel, kept = S("b2", 256, 384), S("b3", 300, 301)

        def mask(p):
            ts(S(rm, P0[p], P0[p] + 128), S("b3" if p else "b0", 0, 128), C(TH + t), None, OP.is_ge)

        def count(p):
            m0, r0, c0 = P0[p], P0[p] + 128, 128 * p
            mms([(firsts(p, 1, 2), S("nbd", 0, 128), S(rm, m0, r0), False, False)])
            mms([(S("b1", c0, c0 + 128), S("lt", 0, 128), S(rm, m0, r0), False, True)])
            scan(S(rm, r0, r0 + 129), S(rm, m0 - 1, r0), S(rm, m0 - 1, r0), S(rm, P0[0] + 256, P0[0] + 257) if p else 0.0, OP.add, OP.max)
            mms([(firsts(p, 0, 2), bd, S(rm, r0, r0 + 128), False, True)])
            if p == last:
                mms([(kept, bd, S(rm, r0 + 128, r0 + 129), True, True)])

        def markers(p):
            act(S("dsb", 128 * p, 128 * p + 128), S("b1", 128 * p, 128 * p + 128), AF.Relu, bias=C(RB))

        def take(p):
            scan(S("pk", 0, 256), S("rs", 0, 256), firsts(p), 0.0, OP.add, OP.max)

        def offsets(p):
            ts(S("off%d" % t, 8 * p, 8 * p + 8), S("pk", 31, 256, 32), -BIG, None, OP.add)

        def scatter(p):
            vscatter(W(dw, M0, M0 + CAP + 128, "off%d" % t, 8 * p, 8 * p + 8), S("dsb", 128 * p, 128 * p + 128))

        def wrap(bank, lo, hi):
            o, i = S(bank, 0, (hi - lo) // 16), int(t > 0)
            mms([(o, win("nxt%de" % i, 0), S("u", lo - 1, hi - 1, 16), True, False)]
                + [(o, win("two%de" % i if k < 15 else "own%de" % i, k), S("u", lo + k, hi, 16), False, k == 15) for k in range(16)])

        def listed(bank, lo, hi):
            ts(S(ls, lo // 16 - 1, hi // 16 - 1), S(bank, 0, (hi - lo) // 16), 15.0 * (128 if t else 1), None, OP.add)

        def pick(eng, lo, hi):
            gather(eng, S(xc, X0 + lo, X0 + hi), W("big", *space, ls, L0 + lo // 16, L0 + hi // 16), -OFS if t else None)

        def left(eng, lo, hi):
            gather(eng, S("gb", lo, hi), W(xc, X0, XZ + 16 if t < 2 else X0 + hi, "lb%d" % t, lo // 16, hi // 16))

        def right(eng, lo, hi):
            gather(eng, S("gc", lo, hi), W(xc, 0, XZ if t < 2 else min(XZ, X0 + hi + HALO), "lc%d" % t, lo // 16, hi // 16))

        def edge(eng):
            gather(eng, S("ge" if t < 2 else "gb", 0, HALO), W(xc, HALO, X0 + HALO, lst, 0, 4))

        def rows(c):
            return range(PARTS[c][0] // 128, PARTS[c][1] // 128)

        def bank(c, k=None, lo=0, hi=128):
            if c == 4:
                return S(MIXB[c], lo, hi)
            return (T[MIXB[c]][:, 0:len(rows(c)), lo:hi] if k is None else T[MIXB[c]][:, k - rows(c)[0], lo:hi]), [(MIXB[c], 0, 512)]

        def offset(c):
            mms([(bank(c), S("idb", 0, 128), S("ones", 0, PARTS[c][1] - PARTS[c][0]), True, False)])

        def mix(c, j):
            lo, hi = PARTS[c]
            if j == 0 and t < 2:
                mms([(bank(c, k), tap(t, 0), S(xc, X0 + k, XZ, 16), False, False) for k in rows(c)])
            else:
                mms([(bank(c), tap(t, j), S(*((xc, X0 + lo, X0 + hi), ("gb", lo, hi), ("gc", lo, hi))[j]), False, j == 2)])

        def centre(c, half):
            lo = X0 + 1024 * half
            mms([(bank(c, k, 64 * half, 64 * half + 64), tap(t, 0), S(xc, lo + k, lo + 1024, 16), False, False) for k in rows(c)])

        def mix_edge(c):
            mms([(bank(c, None, 0, 4), tap(t, 1), S("ge", 4 * rows(c)[0], 4 * rows(c)[-1] + 4), False, False)])

        def near(c):
            lo, hi = PARTS[c]
            ts(S("big", z + lo, z + hi), bank(c), OFS - 15.0, OFS + 15.0, OP.max, OP.min)

        def score(c, stop=False):
            mms([(S("b0", 0, 128), win("sv%d" % (t + 1), k), S("big", z + 128 * k, z + 128 * k + 128), False, stop and k == rows(c)[-1])
                 for k in rows(c)])

        def scores0(c):
            o = S("b0" if c < 2 else "b3", 64 * (c % 2), 64 * (c % 2) + 64)
            mms([(o, win(sv, k), S("big", 1024 * c + k, 1024 * c + 1024, 16), k == 0, k == 15) for k in range(16)])

        def counts():
            for p in range(last + 1):
                cum, m0 = S("b1", 256 + 128 * p, 384 + 128 * p), P0[p]
                mms([(cum, bd, S(rm, m0 + 128, m0 + 256), True, False), (cum, S("ltf", 0, 128), S(rm, m0, m0 + 128), False, False),
                     (cum, S("idk", 0, 128), S(rm, m0, m0 + 128), False, True)])

        if t == 0:
            scores0(0)
            scores0(1)
            preset_firsts(0)
            preset_markers(0)
            scores0(2)
            mask(0)
            small_columns(0)
            count(0)
            place_rows()
            markers(0)
            steps_row()
            list_matrices("v", 0)
            take(0)
            small_columns(1)
            offsets(0)
            scores0(3)
            preset_firsts(1)
            preset_markers(1)
            if PAR.get("early"):
                scatter(0)
            mask(1)
            scaled("v", S("idm", 0, 128), idn, -BIG)
            count(1)
            markers(1)
            if not PAR.get("early"):
                scatter(0)
            take(1)
            scaled("v", S("sv1", 0, 144), e, C(VF + 1))
        else:
            mask(0)
            slots_a(t - 1)
            count(0)
            markers(0)
            shift_lists(t)
            edge_list(t)
            take(0)
            slots_b(t - 1)
        offsets(last)
        ts(S(lse, 0, 5), S("qk", 0, 5), kept, -float(HALO), OP.add, OP.add)
        scatter(last)
        act(C(KS), kept, AF.Copy, bias=float(X0))
        if t < 2:
            act(C(KP), kept, AF.Copy, bias=1.0, scale=-1.0)
        if t == 0:
            scaled("v", S("idk", 0, 128), idn, 8192.0)
            edge_places()
            tap_matrices()
        if t < 2:
            act(S("pen", 0, 128), S("iw", 0, 128), AF.Relu, bias=C(KP))
        cuts = [16] + [M0 + c for c in PAR["cuts"]] + [M0 + CAP]

        def carry(i):
            lo, hi = max(cuts[i], M0), cuts[i + 1]
            scan(S("u", lo, hi), S("dc", 0, hi - lo), S(dw, lo, hi), S("u", lo - 1, lo) if i else 0.0, OP.add, OP.max)

        def leave():
            send(t)
            if t < 2:
                gfill("dw%d" % (t + 1), M0 - 16, M0 + CAP, 0)
            if t == 0:
                shift_lists(0)
                edge_list(0)

        def ahead():
            if t == 0:
                later_constants()
            right_base(t + 1)

        def penalty():
            if t == 0:
                mms([(S("b2", 400, 403), bd, S("vb", 0, 3), True, True)])
            mms([(S("b0", 0, 128), S("idm", 0, 128), S("pen", 0, 128), True, False)])

        def preset():
            preset_firsts(0)
            preset_markers(0)

        ranged = {"p": pick, "l": left, "r": right, "y": lambda eng, lo, hi: store(lo, hi)}
        for level in range(3):
            ranged[str(level)] = lambda eng, lo, hi, level=level: back(eng, level, lo, hi)
        chunked = {"o": offset, "A": lambda c: mix(c, 0), "F": lambda c: centre(c, 0), "G": lambda c: centre(c, 1), "B": lambda c: mix(c, 1),
                   "C": lambda c: mix(c, 2), "E": mix_edge, "n": near, "s": score, "S": lambda c: score(c, True),
                   "u": carry, "W": lambda i: wrap("b%d" % (1 - i % 2), cuts[i], cuts[i + 1]),
                   "L": lambda i: listed("b%d" % (1 - i % 2), cuts[i], cuts[i + 1])}
        named = {"tail": lambda: vcopy(S(dw, 0, TAIL), W(dw, M0 - 16, M0 + CAP, lse, 0, 5)),
                 "utail": lambda: scan(S("u", 0, TAIL), S("dc", 0, TAIL), S(dw, 0, TAIL), 0.0, OP.add, OP.max),
                 "lastv": lambda: gather("v", S(fl, 0, HALO), W("big", *space, ls, 0, 4), -OFS if t else None),
                 "lasta": lambda: gather("a", S(fl, 0, HALO), W("big", *space, ls, 0, 4), -OFS if t else None),
                 "send": leave,
                 "lc1": lambda: ts(lcsel, S("iwd%d" % t, 0, 128), C(KS), C(KS), OP.is_ge, OP.mult),
                 "lc2": lambda: tt(S("lcf", 0, 128), S("iwd%d" % t, 0, 128), lcsel, OP.subtract),
                 "lc3": lambda: vcopy(S("lc%d" % t, 0, 128), S("lcf", 0, 128)),
                 "counts": counts, "slots": lambda: slots_a(t), "slots2": lambda: slots_b(t),
                 "edgev": lambda: edge("v"), "edgea": lambda: edge("a"), "base": ahead, "preset": preset, "pen": penalty}
        for step in PAR["mid" if t < 2 else "end"].split():
            if step in named:
                named[step]()
            elif "-" in step:
                lo, hi = [int(c) for c in step[2:].split("-")]
                mid = (lo + hi) // 32 * 16
                for eng, a, b in (((step[1], lo, hi),) if step[1] != "x" else (("a", lo, mid), ("v", mid, hi))):
                    ranged[step[0]](eng, a, b)
            else:
                for c in step[1:]:
                    chunked[step[0]](int(c))
    tr["finish"]()
